import numpy as np
import ml_dtypes


def mxq(x, axis, fmt="e4m3"):
    dtype, down = {"e4m3": (ml_dtypes.float8_e4m3fn, 7), "e5m2": (ml_dtypes.float8_e5m2, 14)}[fmt]
    v = np.moveaxis(np.asarray(x, np.float32).astype(ml_dtypes.bfloat16).astype(np.float64), axis, -1)
    blocks = v.reshape(v.shape[:-1] + (-1, 32))
    amax = np.abs(blocks).max(-1, keepdims=True)
    byte = np.maximum(np.where(amax > 0, np.frexp(amax)[1] - 1 + 127, 0) - down, 1)
    scale = np.exp2(byte - 127.0)
    codes = (blocks / scale).astype(np.float32).astype(dtype).astype(np.float64)
    return np.moveaxis((codes * scale).reshape(v.shape), -1, axis)


WIDE = False


def mx_kscale(k):
    if not WIDE:
        return np.ones(k)
    levels = np.array([10, -10, 5, -5, 0])
    if k % 512:
        return np.exp2(np.random.permutation(np.resize(levels, k // 32))).repeat(32)
    a = np.empty((k // 512, 16))
    for p in range(k // 512):
        a[p, :8] = np.random.permutation(np.resize(levels, 8))
        for g in range(8):
            far = levels[np.abs(levels - a[p, g]) >= 10]
            a[p, g + 8] = far[np.random.randint(len(far))]
    return np.exp2(a.ravel()).repeat(32)


def f64(x):
    return np.asarray(x).astype(np.float64)


def striped(idx):
    return np.tile(np.asarray(idx).reshape(-1, 16).T, (8, 1)).astype(np.uint16)


def unstriped(offs):
    return offs[:16].T.reshape(-1).astype(np.int64)


E2M1 = np.array([0.0, 0.5, 1.0, 1.5, 2.0, 3.0, 4.0, 6.0, -0.0, -0.5, -1.0, -1.5, -2.0, -3.0, -4.0, -6.0])


def pack_weight(w, fmt):
    k, n = w.shape
    w = f64(np.asarray(w, np.float32).astype(ml_dtypes.bfloat16)).reshape(k // 32, 32, n)
    amax = np.abs(w).max(1)
    if fmt == "e4m3":
        byte = np.frexp(amax)[1] - 1 + 127 - 7
    else:
        mant, ex = np.frexp(amax / 6.0)
        byte = np.where(mant > 0.5, ex, ex - 1) + 127
    byte = np.clip(np.where(amax > 0, byte, 1), 1, 254)
    scaled = (w * np.exp2(127.0 - byte)[:, None, :]).reshape(k, n).astype(np.float32)
    by_word = np.ascontiguousarray(scaled.reshape(k // 512, 128, 4, n).transpose(0, 1, 3, 2))
    if fmt == "e4m3":
        words = by_word.astype(ml_dtypes.float8_e4m3fn).view(np.uint8)
    else:
        c = by_word.astype(ml_dtypes.float4_e2m1fn).view(np.uint8) & 0xF
        words = (c[..., 0::2] | (c[..., 1::2] << 4)).reshape(k // 512, 128, 2 * n)
    return np.ascontiguousarray(words), np.ascontiguousarray(byte.astype(np.uint8).reshape(k // 512, 16, n))


def unpack_weight(words, scales, fmt):
    g, _, n = scales.shape
    words = np.ascontiguousarray(words).reshape(g, 128, n, -1)
    if fmt == "e4m3":
        vals = words.view(ml_dtypes.float8_e4m3fn).astype(np.float64)
    else:
        nib = np.empty((g, 128, n, 4), np.uint8)
        nib[..., 0::2] = words & 0xF
        nib[..., 1::2] = words >> 4
        vals = E2M1[nib]
    vals = vals * np.repeat(np.exp2(scales.astype(np.float64) - 127.0), 8, axis=1)[..., None]
    return vals.transpose(0, 1, 3, 2).reshape(g * 512, n)


B, N, T, D, DV, NQ = 2, 1024, 4096, 1024, 256, 128
PAGE = 512


def setup_inputs():
    n = np.random.standard_normal
    pages = np.random.permutation(T // PAGE)[:B * N // PAGE]
    idx = (pages[:, None] * PAGE + np.arange(PAGE)[None, :]).reshape(-1)
    s = mx_kscale(D)[:, None]
    u = np.ones(T)
    u[idx] = mx_kscale(B * N)
    r = np.random.uniform(0.5, 2.0, T)
    qp = [pack_weight(x, "e4m3") for x in n((B, D, NQ)) * s * (0.60 / np.sqrt(D))]
    k = n((D, T)) / s
    v = n((DV, T)) / (u * r)
    kp = pack_weight(k, "e2m1")
    vp = pack_weight(v.T, "e4m3")
    return {
        "q_words": np.stack([x[0] for x in qp]),
        "q_scales": np.stack([x[1] for x in qp]),
        "k_words": np.ascontiguousarray(kp[0].reshape(D // 1024, 2, 128, T, 2).transpose(0, 2, 3, 1, 4)).reshape(D // 1024, 128, T, 4),
        "k_scales": kp[1],
        "v_words": vp[0],
        "v_scales": vp[1],
        "vs": np.tile(u * r, (128, 1)).astype(np.float32),
        "offs": striped(idx),
        "voffs": striped((pages[:, None] * DV + np.arange(DV)[None, :]).reshape(-1)),
    }


def reference(q_words, q_scales, k_words, k_scales, v_words, v_scales, vs, offs, voffs):
    idx = unstriped(offs)
    k = unpack_weight(k_words.reshape(D // 1024, 128, T, 2, 2).transpose(0, 3, 1, 2, 4).reshape(D // 512, 128, 2 * T), k_scales, "e2m1")
    v = unpack_weight(v_words, v_scales, "e4m3")
    v = v.reshape(T // 512, 512, DV)[unstriped(voffs)[::DV] // DV].reshape(B, N, DV)
    pick = lambda x: x[:, idx].reshape(x.shape[0], B, N).transpose(1, 0, 2)
    q = np.stack([unpack_weight(q_words[b], q_scales[b], "e4m3") for b in range(B)])
    score = q.transpose(0, 2, 1) @ pick(k)
    m = score.max(-1, keepdims=True)
    p = np.exp(score - m)
    total = p.sum(-1, keepdims=True)
    w = p * pick(f64(vs))[:, :1, :]
    y = mxq(w, 2, "e4m3") @ v
    y = y / total
    return y

@@ -1,0 +1,203 @@
+from contextlib import ExitStack
+
+import concourse.mybir as mybir
+from concourse.masks import make_identity
+
+B, N, T, D, DV, NQ = 2, 1024, 4096, 1024, 256, 128
+PAGE = 512
+P = 128
+PASSES = D // 512
+PAGES = B * N // PAGE
+POOL_PAGES = T // PAGE
+FLOPS = 2 * B * NQ * N * (D + DV)
+
+F32 = mybir.dt.float32
+BF16 = mybir.dt.bfloat16
+I32 = mybir.dt.int32
+U32 = mybir.dt.uint32
+U16 = mybir.dt.uint16
+U8 = mybir.dt.uint8
+FP8X4 = mybir.dt.float8_e4m3fn_x4
+FP4X4 = mybir.dt.float4_e2m1fn_x4
+ALU = mybir.AluOpType
+ACT = mybir.ActivationFunctionType
+AX = mybir.AxisListType
+
+V_PLANE = 4
+
+
+def tile_attend_pkv4_qpk_kernel(tc, q_words, q_scales, k_words, k_scales, v_words, v_scales, vs, offs, voffs, out):
+    nc = tc.nc
+    with ExitStack() as ctx:
+        lists = ctx.enter_context(tc.tile_pool(name="lists", bufs=1))
+        keep = ctx.enter_context(tc.tile_pool(name="keep", bufs=1))
+        shared = ctx.enter_context(tc.tile_pool(name="shared", bufs=1))
+        psum = ctx.enter_context(tc.psum_pool(name="psum", bufs=1))
+        turn = ctx.enter_context(tc.psum_pool(name="turn", bufs=2))
+
+        offs_t = lists.tile([P, B * N // 16], U16, name="offs_t")
+        voffs_t = lists.tile([P, PAGES * DV // 16], U16, name="voffs_t")
+        ks_win = shared.tile([P, T // 4], I32, name="ks_win", offset=14336)
+        kw_win = keep.tile([P, T], I32, name="kw_win")
+        nc.sync.dma_start(offs_t[:], offs)
+        nc.sync.dma_start(ks_win[0:32, :], k_scales.rearrange("o f t -> (o f) t").bitcast(I32))
+        nc.sync.dma_start(kw_win[:], k_words[0].rearrange("p t b -> p (t b)").bitcast(I32))
+        nc.sync.dma_start(voffs_t[:], voffs)
+
+        warm = keep.tile([P, 2], F32, name="warm")
+        nc.vector.memset(warm[:, 0:1], 0.0)
+        nc.scalar.activation(warm[:, 1:2], warm[:, 0:1], ACT.Exp)
+
+        vsc_win = keep.tile([P, POOL_PAGES * DV // 4], I32, name="vsc_win")
+        nc.vector.memset(vsc_win[:], 0)
+        nc.vector.memset(ks_win[32:64, :], 0)
+        nc.vector.memset(ks_win[64:128, :], 0)
+        vsc_rows = v_scales.rearrange("u (g r) e -> r g u e", r=4)
+        for r in range(4):
+            nc.scalar.dma_start(vsc_win[V_PLANE + r : P : 32, :].rearrange("p (u e) -> p u e", u=POOL_PAGES), vsc_rows[r].bitcast(I32))
+
+        q_plane = keep.tile([P, B * PASSES, NQ // 4], I32, name="q_plane", align_bytes=64)
+        nc.gpsimd.memset(q_plane[:], 0)
+        qs_rows = q_scales.rearrange("b o (g r) q -> r g (b o) q", r=4)
+        for r in range(4):
+            nc.gpsimd.dma_start(q_plane[r:P:32, :, :], qs_rows[r].bitcast(I32))
+        ident = keep.tile([P, P], F32, name="ident")
+        make_identity(nc, ident[:])
+
+        q_codes = keep.tile([P, B * PASSES, NQ], I32, name="q_codes", align_bytes=64)
+        nc.sync.dma_start(q_codes[:], q_words.rearrange("b o p q t -> p (b o) (q t)").bitcast(I32))
+
+        k_plane = keep.tile([P, PASSES, B * N // 4], I32, name="k_plane", align_bytes=64)
+        nc.vector.memset(k_plane[:], 0)
+        ks_got = keep.tile([P, B * N], U8, name="ks_got")
+        nc.vector.tensor_copy(ks_got[:], ks_win[:].bitcast(U8).indirect(offs_t[:]))
+        for o in range(PASSES):
+            for r in range(4):
+                (nc.sync, nc.scalar)[o].dma_start(k_plane[r:P:32, o, :], ks_got[16 * o + r : 16 * o + 16 : 4, :].bitcast(I32))
+
+        vs_win = shared.tile([P, T], F32, name="vs_win", offset=0)
+        nc.sync.dma_start(vs_win[:], vs)
+        vw_win = shared.tile([P, POOL_PAGES * DV], I32, name="vw_win", offset=16384)
+        nc.sync.dma_start(
+            vw_win[:].rearrange("p (u e) -> p u e", u=POOL_PAGES),
+            v_words.rearrange("u p e r -> p u (e r)").bitcast(I32),
+        )
+
+        v_plane = keep.tile([P, PAGES * DV], U8, name="v_plane", align_bytes=64)
+        nc.vector.tensor_copy(v_plane[:], vsc_win[:].bitcast(U8).indirect(voffs_t[:]))
+
+        def page_list(g):
+            return offs_t[:, g * PAGE // 16 : (g + 1) * PAGE // 16]
+
+        scores = [psum.tile([P, PAGE], F32, name="scores%d" % g) for g in range(PAGES)]
+        k_got = [keep.tile([P, PAGE], U32, name="k_got%d" % g) for g in range(PAGES)]
+        k_pass = [keep.tile([P, PASSES, 2 * PAGE], U8, name="k_pass%d" % g, align_bytes=64) for g in range(PAGES)]
+
+        def gather_keys(g):
+            nc.vector.tensor_copy(k_got[g][:], kw_win[:].bitcast(U32).indirect(page_list(g)))
+
+        def score(g):
+            b = g // 2
+            nc.vector.tensor_copy(k_pass[g][:].bitcast(U16), k_got[g][:].bitcast(U16).rearrange("p (n o) -> p o n", o=PASSES))
+            for o in range(PASSES):
+                nc.tensor.matmul_mx(
+                    out=scores[g][:],
+                    lhsT=q_codes[:, b * PASSES + o, :].bitcast(FP8X4),
+                    lhsT_scale=q_plane[:, b * PASSES + o, :].bitcast(U8),
+                    rhs=k_pass[g][:, o, :].bitcast(FP4X4),
+                    rhs_scale=k_plane[:, o, g * PAGE // 4 : (g + 1) * PAGE // 4].bitcast(U8),
+                    start=(o == 0),
+                    stop=(o == PASSES - 1),
+                )
+
+        gather_keys(0)
+        gather_keys(1)
+        score(0)
+        gather_keys(2)
+        score(1)
+        gather_keys(3)
+        score(2)
+        score(3)
+
+        page_max = [keep.tile([P, 2], F32, name="page_max%d" % b) for b in range(B)]
+        neg_max = [keep.tile([P, 1], F32, name="neg_max%d" % b) for b in range(B)]
+        sums = keep.tile([P, 2, B], F32, name="sums")
+        p = [keep.tile([P, PAGE], F32, name="p%d" % g, tag="p%d" % g, align_bytes=64) for g in range(PAGES)]
+
+        def row_max(g):
+            b, j = divmod(g, 2)
+            nc.vector.tensor_reduce(page_max[b][:, j : j + 1], scores[g][:], AX.X, ALU.max, negate=True)
+
+        def exps(b):
+            nc.vector.tensor_tensor(neg_max[b][:], page_max[b][:, 0:1], page_max[b][:, 1:2], ALU.min)
+            for j in range(2):
+                nc.scalar.activation(
+                    p[2 * b + j][:], scores[2 * b + j][:], ACT.Exp,
+                    bias=neg_max[b][:], accum_out=sums[:, j, b : b + 1],
+                )
+
+        row_max(0)
+        row_max(1)
+        row_max(2)
+        exps(0)
+        row_max(3)
+        exps(1)
+
+        w32 = [keep.tile([P, PAGE], F32, name="w32_%d" % g) for g in range(PAGES)]
+        w_t = [keep.tile([P, PAGE], BF16, name="w_t%d" % g, align_bytes=64) for g in range(PAGES)]
+        total = keep.tile([P, B], F32, name="total")
+        inv = keep.tile([P, B], F32, name="inv")
+
+        def weigh(g):
+            nc.vector.tensor_tensor(w32[g][:], vs_win[:].indirect(page_list(g)), p[g][:], ALU.mult)
+
+        def turn_f32(g):
+            bank = turn.tile([P, 4, NQ], F32, name="bank")
+            for t in range(4):
+                nc.tensor.transpose(bank[:, t, :], w32[g][:, t:PAGE:4], ident[:])
+            nc.scalar.copy(w_t[g][:].rearrange("p (q t) -> p q t", t=4), bank[:].rearrange("p t q -> p q t"))
+
+        def turn_pairs(g, w16):
+            pairs = w16[:].bitcast(F32)
+            bank = turn.tile([P, 4, NQ], F32, name="bank")
+            for u in range(2):
+                nc.tensor.transpose(bank[:, u, :], pairs[:, u : PAGE // 2 : 2], ident[:])
+            nc.scalar.copy(w_t[g][:].bitcast(F32).rearrange("p (q u) -> p q u", u=2), bank[:, 0:2, :].rearrange("p u q -> p q u"))
+
+        w16 = [keep.tile([P, PAGE], BF16, name="w16_%d" % j) for j in range(2)]
+        for g in range(PAGES):
+            weigh(g)
+        nc.scalar.copy(w16[0][:], w32[2][:])
+        nc.vector.tensor_tensor(total[:], sums[:, 0, :], sums[:, 1, :], ALU.add)
+        nc.vector.tensor_copy(w16[1][:], w32[3][:])
+        turn_f32(0)
+        turn_f32(1)
+        turn_pairs(2, w16[0])
+        turn_pairs(3, w16[1])
+
+        v_got = [keep.tile([P, 2 * DV], U32, name="v_got%d" % b, tag="p%d" % (2 + b), align_bytes=64) for b in range(B)]
+        for b in range(B):
+            nc.vector.tensor_copy(v_got[b][:], vw_win[:].bitcast(U32).indirect(voffs_t[:, b * 32 : (b + 1) * 32]))
+            if b == 0:
+                nc.vector.reciprocal(inv[:], total[:])
+            acc = psum.tile([P, DV], F32, name="acc%d" % b)
+            for j in range(2):
+                g = 2 * b + j
+                w_codes = keep.tile([P, NQ], U32, name="w_codes%d" % g, align_bytes=64)
+                w_plane = keep.tile([P, NQ], U8, name="w_plane%d" % g, align_bytes=64)
+                nc.vector.quantize_mx(out=w_codes[:].bitcast(FP8X4), scales=w_plane[:], in_=w_t[g][:])
+                nc.tensor.matmul_mx(
+                    out=acc[:],
+                    lhsT=w_codes[:].bitcast(FP8X4),
+                    lhsT_scale=w_plane[:],
+                    rhs=v_got[b][:, j * DV : (j + 1) * DV].bitcast(FP8X4),
+                    rhs_scale=v_plane[V_PLANE:P, g * DV : (g + 1) * DV],
+                    start=(j == 0),
+                    stop=(j == 1),
+                )
+            y = keep.tile([P, DV], F32, name="y%d" % b)
+            if b == 0:
+                nc.scalar.activation(y[:], acc[:], ACT.Copy, scale=inv[:, b : b + 1])
+            else:
+                nc.vector.tensor_scalar(y[:], acc[:], inv[:, b : b + 1], None, ALU.mult)
+            nc.sync.dma_start(out[b], y[:])

@@ -40,13 +40,9 @@ def tile_attend_pkv4_qpk_kernel(tc, q_words, q_scales, k_words, k_scales, v_word
         ks_win = shared.tile([P, T // 4], I32, name="ks_win", offset=14336)
         kw_win = keep.tile([P, T], I32, name="kw_win")
         nc.sync.dma_start(offs_t[:], offs)
-        nc.sync.dma_start(ks_win[0:32, :], k_scales.rearrange("o f t -> (o f) t").bitcast(I32))
-        nc.sync.dma_start(kw_win[:], k_words[0].rearrange("p t b -> p (t b)").bitcast(I32))
         nc.sync.dma_start(voffs_t[:], voffs)
-
-        warm = keep.tile([P, 2], F32, name="warm")
-        nc.vector.memset(warm[:, 0:1], 0.0)
-        nc.scalar.activation(warm[:, 1:2], warm[:, 0:1], ACT.Exp)
+        nc.scalar.dma_start(ks_win[0:32, :], k_scales.rearrange("o f t -> (o f) t").bitcast(I32))
+        nc.sync.dma_start(kw_win[:], k_words[0].rearrange("p t b -> p (t b)").bitcast(I32))
 
         vsc_win = keep.tile([P, POOL_PAGES * DV // 4], I32, name="vsc_win")
         nc.vector.memset(vsc_win[:], 0)
@@ -57,7 +53,7 @@ def tile_attend_pkv4_qpk_kernel(tc, q_words, q_scales, k_words, k_scales, v_word
             nc.scalar.dma_start(vsc_win[V_PLANE + r : P : 32, :].rearrange("p (u e) -> p u e", u=POOL_PAGES), vsc_rows[r].bitcast(I32))
 
         q_plane = keep.tile([P, B * PASSES, NQ // 4], I32, name="q_plane", align_bytes=64)
-        nc.gpsimd.memset(q_plane[:], 0)
+        nc.vector.memset(q_plane[:], 0)
         qs_rows = q_scales.rearrange("b o (g r) q -> r g (b o) q", r=4)
         for r in range(4):
             nc.gpsimd.dma_start(q_plane[r:P:32, :, :], qs_rows[r].bitcast(I32))
@@ -69,6 +65,10 @@ def tile_attend_pkv4_qpk_kernel(tc, q_words, q_scales, k_words, k_scales, v_word
 
         k_plane = keep.tile([P, PASSES, B * N // 4], I32, name="k_plane", align_bytes=64)
         nc.vector.memset(k_plane[:], 0)
+        warm = keep.tile([P, 2], F32, name="warm")
+        nc.vector.memset(warm[:, 0:1], 0.0)
+        nc.scalar.activation(warm[:, 1:2], warm[:, 0:1], ACT.Exp)
+
         ks_got = keep.tile([P, B * N], U8, name="ks_got")
         nc.vector.tensor_copy(ks_got[:], ks_win[:].bitcast(U8).indirect(offs_t[:]))
         for o in range(PASSES):
@@ -164,16 +164,16 @@ def tile_attend_pkv4_qpk_kernel(tc, q_words, q_scales, k_words, k_scales, v_word
                 nc.tensor.transpose(bank[:, u, :], pairs[:, u : PAGE // 2 : 2], ident[:])
             nc.scalar.copy(w_t[g][:].bitcast(F32).rearrange("p (q u) -> p q u", u=2), bank[:, 0:2, :].rearrange("p u q -> p q u"))
 
-        w16 = [keep.tile([P, PAGE], BF16, name="w16_%d" % j) for j in range(2)]
+        w16 = {g: keep.tile([P, PAGE], BF16, name="w16_%d" % g) for g in range(1, PAGES)}
         for g in range(PAGES):
             weigh(g)
-        nc.scalar.copy(w16[0][:], w32[2][:])
+        nc.scalar.copy(w16[1][:], w32[1][:])
+        nc.scalar.copy(w16[2][:], w32[2][:])
         nc.vector.tensor_tensor(total[:], sums[:, 0, :], sums[:, 1, :], ALU.add)
-        nc.vector.tensor_copy(w16[1][:], w32[3][:])
+        nc.vector.tensor_copy(w16[3][:], w32[3][:])
         turn_f32(0)
-        turn_f32(1)
-        turn_pairs(2, w16[0])
-        turn_pairs(3, w16[1])
+        for g in range(1, PAGES):
+            turn_pairs(g, w16[g])
 
         v_got = [keep.tile([P, 2 * DV], U32, name="v_got%d" % b, tag="p%d" % (2 + b), align_bytes=64) for b in range(B)]
         for b in range(B):

@@ -24,6 +24,11 @@ ACT = mybir.ActivationFunctionType
 AX = mybir.AxisListType
 
 V_PLANE = 4
+KW_LOADS = 4
+VS_AT = 0
+Q_AT = VS_AT + 4 * T
+VW_AT = Q_AT + 4 * B * PASSES * NQ
+KS_AT = Q_AT - 1024
 
 
 def tile_attend_pkv4_qpk_kernel(tc, q_words, q_scales, k_words, k_scales, v_words, v_scales, vs, offs, voffs, out):
@@ -37,17 +42,18 @@ def tile_attend_pkv4_qpk_kernel(tc, q_words, q_scales, k_words, k_scales, v_word
 
         offs_t = lists.tile([P, B * N // 16], U16, name="offs_t")
         voffs_t = lists.tile([P, PAGES * DV // 16], U16, name="voffs_t")
-        ks_win = shared.tile([P, T // 4], I32, name="ks_win", offset=14336)
+        ks_win = shared.tile([P, T // 4], I32, name="ks_win", offset=KS_AT)
         kw_win = keep.tile([P, T], I32, name="kw_win")
         nc.sync.dma_start(offs_t[:], offs)
         nc.sync.dma_start(voffs_t[:], voffs)
-        nc.scalar.dma_start(ks_win[0:32, :], k_scales.rearrange("o f t -> (o f) t").bitcast(I32))
-        nc.sync.dma_start(kw_win[:], k_words[0].rearrange("p t b -> p (t b)").bitcast(I32))
+        nc.sync.dma_start(ks_win[0:32, :], k_scales.rearrange("o f t -> (o f) t").bitcast(I32))
+        kw_rows = k_words[0].rearrange("p t b -> p (t b)").bitcast(I32)
+        for c in range(KW_LOADS):
+            cols = slice(c * T // KW_LOADS, (c + 1) * T // KW_LOADS)
+            nc.sync.dma_start(kw_win[:, cols], kw_rows[:, cols])
 
         vsc_win = keep.tile([P, POOL_PAGES * DV // 4], I32, name="vsc_win")
         nc.vector.memset(vsc_win[:], 0)
-        nc.vector.memset(ks_win[32:64, :], 0)
-        nc.vector.memset(ks_win[64:128, :], 0)
         vsc_rows = v_scales.rearrange("u (g r) e -> r g u e", r=4)
         for r in range(4):
             nc.scalar.dma_start(vsc_win[V_PLANE + r : P : 32, :].rearrange("p (u e) -> p u e", u=POOL_PAGES), vsc_rows[r].bitcast(I32))
@@ -56,28 +62,30 @@ def tile_attend_pkv4_qpk_kernel(tc, q_words, q_scales, k_words, k_scales, v_word
         nc.vector.memset(q_plane[:], 0)
         qs_rows = q_scales.rearrange("b o (g r) q -> r g (b o) q", r=4)
         for r in range(4):
-            nc.gpsimd.dma_start(q_plane[r:P:32, :, :], qs_rows[r].bitcast(I32))
+            nc.scalar.dma_start(q_plane[r:P:32, :, :], qs_rows[r].bitcast(I32))
+
+        nc.vector.memset(ks_win[32:64, :], 0)
+        nc.gpsimd.memset(ks_win[64:128, :], 0)
         ident = keep.tile([P, P], F32, name="ident")
         make_identity(nc, ident[:])
 
-        q_codes = keep.tile([P, B * PASSES, NQ], I32, name="q_codes", align_bytes=64)
-        nc.sync.dma_start(q_codes[:], q_words.rearrange("b o p q t -> p (b o) (q t)").bitcast(I32))
-
         k_plane = keep.tile([P, PASSES, B * N // 4], I32, name="k_plane", align_bytes=64)
-        nc.vector.memset(k_plane[:], 0)
+        nc.gpsimd.memset(k_plane[:], 0)
         warm = keep.tile([P, 2], F32, name="warm")
         nc.vector.memset(warm[:, 0:1], 0.0)
         nc.scalar.activation(warm[:, 1:2], warm[:, 0:1], ACT.Exp)
 
         ks_got = keep.tile([P, B * N], U8, name="ks_got")
         nc.vector.tensor_copy(ks_got[:], ks_win[:].bitcast(U8).indirect(offs_t[:]))
+        q_codes = shared.tile([P, B * PASSES, NQ], I32, name="q_codes", align_bytes=64, offset=Q_AT)
+        nc.sync.dma_start(q_codes[:], q_words.rearrange("b o p q t -> p (b o) (q t)").bitcast(I32))
         for o in range(PASSES):
             for r in range(4):
-                (nc.sync, nc.scalar)[o].dma_start(k_plane[r:P:32, o, :], ks_got[16 * o + r : 16 * o + 16 : 4, :].bitcast(I32))
+                nc.sync.dma_start(k_plane[r:P:32, o, :], ks_got[16 * o + r : 16 * o + 16 : 4, :].bitcast(I32))
 
-        vs_win = shared.tile([P, T], F32, name="vs_win", offset=0)
+        vs_win = shared.tile([P, T], F32, name="vs_win", offset=VS_AT)
         nc.sync.dma_start(vs_win[:], vs)
-        vw_win = shared.tile([P, POOL_PAGES * DV], I32, name="vw_win", offset=16384)
+        vw_win = shared.tile([P, POOL_PAGES * DV], I32, name="vw_win", offset=VW_AT)
         nc.sync.dma_start(
             vw_win[:].rearrange("p (u e) -> p u e", u=POOL_PAGES),
             v_words.rearrange("u p e r -> p u (e r)").bitcast(I32),

@@ -21,14 +21,15 @@ FP8X4 = mybir.dt.float8_e4m3fn_x4
 FP4X4 = mybir.dt.float4_e2m1fn_x4
 ALU = mybir.AluOpType
 ACT = mybir.ActivationFunctionType
-AX = mybir.AxisListType
 
 V_PLANE = 4
-KW_LOADS = 4
+EDGE = 64
 VS_AT = 0
-Q_AT = VS_AT + 4 * T
-VW_AT = Q_AT + 4 * B * PASSES * NQ
-KS_AT = Q_AT - 1024
+KS_TILE_AT = VS_AT + 4 * T - EDGE
+KS_AT = KS_TILE_AT + EDGE
+VW_AT = KS_AT + T
+WT_AT = VW_AT + 4 * POOL_PAGES * DV
+BANK = 2048
 
 
 def tile_attend_pkv4_qpk_kernel(tc, q_words, q_scales, k_words, k_scales, v_words, v_scales, vs, offs, voffs, out):
@@ -38,19 +39,18 @@ def tile_attend_pkv4_qpk_kernel(tc, q_words, q_scales, k_words, k_scales, v_word
         keep = ctx.enter_context(tc.tile_pool(name="keep", bufs=1))
         shared = ctx.enter_context(tc.tile_pool(name="shared", bufs=1))
         psum = ctx.enter_context(tc.psum_pool(name="psum", bufs=1))
-        turn = ctx.enter_context(tc.psum_pool(name="turn", bufs=2))
 
         offs_t = lists.tile([P, B * N // 16], U16, name="offs_t")
         voffs_t = lists.tile([P, PAGES * DV // 16], U16, name="voffs_t")
-        ks_win = shared.tile([P, T // 4], I32, name="ks_win", offset=KS_AT)
+        ks_tile = shared.tile([P, (T + 2 * EDGE) // 4], I32, name="ks_tile", align_bytes=64, offset=KS_TILE_AT)
+        ks_win = ks_tile[:, EDGE // 4 : (EDGE + T) // 4]
         kw_win = keep.tile([P, T], I32, name="kw_win")
+        q_codes = keep.tile([P, B * PASSES, NQ], I32, name="q_codes", align_bytes=64)
         nc.sync.dma_start(offs_t[:], offs)
+        nc.sync.dma_start(ks_win[0:32, :], k_scales.rearrange("o f t -> f o t").bitcast(I32))
         nc.sync.dma_start(voffs_t[:], voffs)
-        nc.sync.dma_start(ks_win[0:32, :], k_scales.rearrange("o f t -> (o f) t").bitcast(I32))
-        kw_rows = k_words[0].rearrange("p t b -> p (t b)").bitcast(I32)
-        for c in range(KW_LOADS):
-            cols = slice(c * T // KW_LOADS, (c + 1) * T // KW_LOADS)
-            nc.sync.dma_start(kw_win[:, cols], kw_rows[:, cols])
+        nc.sync.dma_start(kw_win[:], k_words[0].rearrange("p t b -> p (t b)").bitcast(I32))
+        nc.sync.dma_start(q_codes[:], q_words.rearrange("b o p q t -> p (b o) (q t)").bitcast(I32))
 
         vsc_win = keep.tile([P, POOL_PAGES * DV // 4], I32, name="vsc_win")
         nc.vector.memset(vsc_win[:], 0)
@@ -65,27 +65,18 @@ def tile_attend_pkv4_qpk_kernel(tc, q_words, q_scales, k_words, k_scales, v_word
             nc.scalar.dma_start(q_plane[r:P:32, :, :], qs_rows[r].bitcast(I32))
 
         nc.vector.memset(ks_win[32:64, :], 0)
-        nc.gpsimd.memset(ks_win[64:128, :], 0)
+        nc.vector.memset(ks_win[64:128, :], 0)
         ident = keep.tile([P, P], F32, name="ident")
         make_identity(nc, ident[:])
 
-        k_plane = keep.tile([P, PASSES, B * N // 4], I32, name="k_plane", align_bytes=64)
-        nc.gpsimd.memset(k_plane[:], 0)
-        warm = keep.tile([P, 2], F32, name="warm")
-        nc.vector.memset(warm[:, 0:1], 0.0)
-        nc.scalar.activation(warm[:, 1:2], warm[:, 0:1], ACT.Exp)
-
         ks_got = keep.tile([P, B * N], U8, name="ks_got")
-        nc.vector.tensor_copy(ks_got[:], ks_win[:].bitcast(U8).indirect(offs_t[:]))
-        q_codes = shared.tile([P, B * PASSES, NQ], I32, name="q_codes", align_bytes=64, offset=Q_AT)
-        nc.sync.dma_start(q_codes[:], q_words.rearrange("b o p q t -> p (b o) (q t)").bitcast(I32))
-        for o in range(PASSES):
-            for r in range(4):
-                nc.sync.dma_start(k_plane[r:P:32, o, :], ks_got[16 * o + r : 16 * o + 16 : 4, :].bitcast(I32))
-
-        vs_win = shared.tile([P, T], F32, name="vs_win", offset=VS_AT)
+        nc.vector.tensor_copy(ks_got[:], ks_win.bitcast(U8).indirect(offs_t[:]))
+        k_plane = shared.tile([P, PASSES, B * N // 4], I32, name="k_plane", align_bytes=64, offset=KS_AT)
+        for quad in range(4):
+            nc.sync.dma_start(k_plane[32 * quad : 32 * quad + 4, :, :], ks_got[8 * quad : 8 * quad + 8, :].bitcast(I32))
+        vs_win = shared.tile([P, T], F32, name="vs_win", align_bytes=64, offset=VS_AT)
         nc.sync.dma_start(vs_win[:], vs)
-        vw_win = shared.tile([P, POOL_PAGES * DV], I32, name="vw_win", offset=VW_AT)
+        vw_win = shared.tile([P, POOL_PAGES * DV], I32, name="vw_win", align_bytes=64, offset=VW_AT)
         nc.sync.dma_start(
             vw_win[:].rearrange("p (u e) -> p u e", u=POOL_PAGES),
             v_words.rearrange("u p e r -> p u (e r)").bitcast(I32),
@@ -97,26 +88,41 @@ def tile_attend_pkv4_qpk_kernel(tc, q_words, q_scales, k_words, k_scales, v_word
         def page_list(g):
             return offs_t[:, g * PAGE // 16 : (g + 1) * PAGE // 16]
 
-        scores = [psum.tile([P, PAGE], F32, name="scores%d" % g) for g in range(PAGES)]
+        scores = [psum.tile([P, PAGE], F32, name="scores%d" % g, offset=g * BANK) for g in range(PAGES)]
         k_got = [keep.tile([P, PAGE], U32, name="k_got%d" % g) for g in range(PAGES)]
-        k_pass = [keep.tile([P, PASSES, 2 * PAGE], U8, name="k_pass%d" % g, align_bytes=64) for g in range(PAGES)]
+        neg_score = [keep.tile([P, PAGE], F32, name="neg_score%d" % g) for g in range(PAGES)]
+        neg_max = [keep.tile([P, 1], F32, name="neg_max%d" % g) for g in range(PAGES)]
+        p = [keep.tile([P, PAGE], F32, name="p%d" % g, tag="p%d" % g, align_bytes=64) for g in range(PAGES)]
+        sums = keep.tile([P, 2, B], F32, name="sums")
 
         def gather_keys(g):
             nc.vector.tensor_copy(k_got[g][:], kw_win[:].bitcast(U32).indirect(page_list(g)))
 
         def score(g):
             b = g // 2
-            nc.vector.tensor_copy(k_pass[g][:].bitcast(U16), k_got[g][:].bitcast(U16).rearrange("p (n o) -> p o n", o=PASSES))
+            k_pass = keep.tile([P, PASSES, 2 * PAGE], U8, name="k_pass%d" % g, tag="k_pass%d" % (g % 3), align_bytes=64)
+            nc.vector.tensor_copy(k_pass[:].bitcast(U16), k_got[g][:].bitcast(U16).rearrange("p (n o) -> p o n", o=PASSES))
             for o in range(PASSES):
                 nc.tensor.matmul_mx(
                     out=scores[g][:],
                     lhsT=q_codes[:, b * PASSES + o, :].bitcast(FP8X4),
                     lhsT_scale=q_plane[:, b * PASSES + o, :].bitcast(U8),
-                    rhs=k_pass[g][:, o, :].bitcast(FP4X4),
+                    rhs=k_pass[:, o, :].bitcast(FP4X4),
                     rhs_scale=k_plane[:, o, g * PAGE // 4 : (g + 1) * PAGE // 4].bitcast(U8),
                     start=(o == 0),
                     stop=(o == PASSES - 1),
                 )
+
+        def row_max(g):
+            nc.vector.tensor_scalar(
+                neg_score[g][:], scores[g][:], -1.0, neg_max[g - 1][:] if g % 2 else None,
+                ALU.mult, ALU.min, accum_out=neg_max[g][:],
+            )
+
+        def exps(b):
+            for j in range(2):
+                g = 2 * b + j
+                nc.scalar.activation(p[g][:], neg_score[g][:], ACT.Exp, bias=neg_max[2 * b + 1][:], scale=-1.0, accum_out=sums[:, j, b : b + 1])
 
         gather_keys(0)
         gather_keys(1)
@@ -125,79 +131,53 @@ def tile_attend_pkv4_qpk_kernel(tc, q_words, q_scales, k_words, k_scales, v_word
         score(1)
         gather_keys(3)
         score(2)
-        score(3)
-
-        page_max = [keep.tile([P, 2], F32, name="page_max%d" % b) for b in range(B)]
-        neg_max = [keep.tile([P, 1], F32, name="neg_max%d" % b) for b in range(B)]
-        sums = keep.tile([P, 2, B], F32, name="sums")
-        p = [keep.tile([P, PAGE], F32, name="p%d" % g, tag="p%d" % g, align_bytes=64) for g in range(PAGES)]
-
-        def row_max(g):
-            b, j = divmod(g, 2)
-            nc.vector.tensor_reduce(page_max[b][:, j : j + 1], scores[g][:], AX.X, ALU.max, negate=True)
-
-        def exps(b):
-            nc.vector.tensor_tensor(neg_max[b][:], page_max[b][:, 0:1], page_max[b][:, 1:2], ALU.min)
-            for j in range(2):
-                nc.scalar.activation(
-                    p[2 * b + j][:], scores[2 * b + j][:], ACT.Exp,
-                    bias=neg_max[b][:], accum_out=sums[:, j, b : b + 1],
-                )
-
         row_max(0)
+        score(3)
         row_max(1)
-        row_max(2)
         exps(0)
+        row_max(2)
         row_max(3)
         exps(1)
 
-        w32 = [keep.tile([P, PAGE], F32, name="w32_%d" % g) for g in range(PAGES)]
-        w_t = [keep.tile([P, PAGE], BF16, name="w_t%d" % g, align_bytes=64) for g in range(PAGES)]
+        w_t = [shared.tile([P, PAGE], BF16, name="w_t%d" % g, align_bytes=64, offset=WT_AT + (0, 1, 3, 4)[g] * 2 * PAGE) for g in range(PAGES)]
+        for g in range(PAGES):
+            w32 = keep.tile([P, PAGE], F32, name="w32_%d" % g)
+            nc.vector.tensor_tensor(w32[:], vs_win[:].indirect(page_list(g)), p[g][:], ALU.mult)
+            w16 = keep.tile([P, PAGE], BF16, name="w16_%d" % g)
+            nc.scalar.copy(w16[:].rearrange("p (u s e) -> p u s e", u=2, e=2), w32[:].rearrange("p (s u e) -> p u s e", u=2, e=2))
+            bank = psum.tile([P, 2, NQ], F32, name="bank%d" % g, offset=(4 + g % 2) * BANK)
+            for u in range(2):
+                nc.tensor.transpose(bank[:, u, :], w16[:].bitcast(F32)[:, u * P : (u + 1) * P], ident[:])
+            nc.scalar.copy(w_t[g][:].bitcast(F32).rearrange("p (q u) -> p q u", u=2), bank[:].rearrange("p u q -> p q u"))
+
         total = keep.tile([P, B], F32, name="total")
         inv = keep.tile([P, B], F32, name="inv")
-
-        def weigh(g):
-            nc.vector.tensor_tensor(w32[g][:], vs_win[:].indirect(page_list(g)), p[g][:], ALU.mult)
-
-        def turn_f32(g):
-            bank = turn.tile([P, 4, NQ], F32, name="bank")
-            for t in range(4):
-                nc.tensor.transpose(bank[:, t, :], w32[g][:, t:PAGE:4], ident[:])
-            nc.scalar.copy(w_t[g][:].rearrange("p (q t) -> p q t", t=4), bank[:].rearrange("p t q -> p q t"))
-
-        def turn_pairs(g, w16):
-            pairs = w16[:].bitcast(F32)
-            bank = turn.tile([P, 4, NQ], F32, name="bank")
-            for u in range(2):
-                nc.tensor.transpose(bank[:, u, :], pairs[:, u : PAGE // 2 : 2], ident[:])
-            nc.scalar.copy(w_t[g][:].bitcast(F32).rearrange("p (q u) -> p q u", u=2), bank[:, 0:2, :].rearrange("p u q -> p q u"))
-
-        w16 = {g: keep.tile([P, PAGE], BF16, name="w16_%d" % g) for g in range(1, PAGES)}
-        for g in range(PAGES):
-            weigh(g)
-        nc.scalar.copy(w16[1][:], w32[1][:])
-        nc.scalar.copy(w16[2][:], w32[2][:])
         nc.vector.tensor_tensor(total[:], sums[:, 0, :], sums[:, 1, :], ALU.add)
-        nc.vector.tensor_copy(w16[3][:], w32[3][:])
-        turn_f32(0)
-        for g in range(1, PAGES):
-            turn_pairs(g, w16[g])
+        w_codes = [keep.tile([P, NQ], U32, name="w_codes%d" % g, align_bytes=64) for g in range(PAGES)]
+        w_plane = [keep.tile([P, NQ], U8, name="w_plane%d" % g, align_bytes=64) for g in range(PAGES)]
 
-        v_got = [keep.tile([P, 2 * DV], U32, name="v_got%d" % b, tag="p%d" % (2 + b), align_bytes=64) for b in range(B)]
+        def quantise(g):
+            nc.vector.quantize_mx(out=w_codes[g][:].bitcast(FP8X4), scales=w_plane[g][:], in_=w_t[g][:])
+
+        def gather_values(b, got):
+            nc.vector.tensor_copy(got[:], vw_win[:].bitcast(U32).indirect(voffs_t[:, b * 32 : (b + 1) * 32]))
+            return got
+
+        v_got = [gather_values(0, keep.tile([P, 2 * DV], U32, name="v_got0", tag="p2", align_bytes=64))]
+        quantise(0)
+        nc.vector.reciprocal(inv[:], total[:])
+        quantise(1)
+        quantise(2)
+        v_got.append(gather_values(1, shared.tile([P, 2 * DV], U32, name="v_got1", align_bytes=64, offset=WT_AT + 2 * PAGE)))
+        quantise(3)
         for b in range(B):
-            nc.vector.tensor_copy(v_got[b][:], vw_win[:].bitcast(U32).indirect(voffs_t[:, b * 32 : (b + 1) * 32]))
-            if b == 0:
-                nc.vector.reciprocal(inv[:], total[:])
-            acc = psum.tile([P, DV], F32, name="acc%d" % b)
+            acc = psum.tile([P, DV], F32, name="acc%d" % b, offset=(5 + b) * BANK)
             for j in range(2):
                 g = 2 * b + j
-                w_codes = keep.tile([P, NQ], U32, name="w_codes%d" % g, align_bytes=64)
-                w_plane = keep.tile([P, NQ], U8, name="w_plane%d" % g, align_bytes=64)
-                nc.vector.quantize_mx(out=w_codes[:].bitcast(FP8X4), scales=w_plane[:], in_=w_t[g][:])
                 nc.tensor.matmul_mx(
                     out=acc[:],
-                    lhsT=w_codes[:].bitcast(FP8X4),
-                    lhsT_scale=w_plane[:],
+                    lhsT=w_codes[g][:].bitcast(FP8X4),
+                    lhsT_scale=w_plane[g][:],
                     rhs=v_got[b][:, j * DV : (j + 1) * DV].bitcast(FP8X4),
                     rhs_scale=v_plane[V_PLANE:P, g * DV : (g + 1) * DV],
                     start=(j == 0),

@@ -65,14 +65,14 @@ def tile_attend_pkv4_qpk_kernel(tc, q_words, q_scales, k_words, k_scales, v_word
             nc.scalar.dma_start(q_plane[r:P:32, :, :], qs_rows[r].bitcast(I32))
 
         nc.vector.memset(ks_win[32:64, :], 0)
-        nc.vector.memset(ks_win[64:128, :], 0)
+        nc.gpsimd.memset(ks_win[64:128, :], 0)
         ident = keep.tile([P, P], F32, name="ident")
         make_identity(nc, ident[:])
 
         ks_got = keep.tile([P, B * N], U8, name="ks_got")
         nc.vector.tensor_copy(ks_got[:], ks_win.bitcast(U8).indirect(offs_t[:]))
         k_plane = shared.tile([P, PASSES, B * N // 4], I32, name="k_plane", align_bytes=64, offset=KS_AT)
-        for quad in range(4):
+        for quad in (0, 2, 1, 3):
             nc.sync.dma_start(k_plane[32 * quad : 32 * quad + 4, :, :], ks_got[8 * quad : 8 * quad + 8, :].bitcast(I32))
         vs_win = shared.tile([P, T], F32, name="vs_win", align_bytes=64, offset=VS_AT)
         nc.sync.dma_start(vs_win[:], vs)
@@ -140,14 +140,21 @@ def tile_attend_pkv4_qpk_kernel(tc, q_words, q_scales, k_words, k_scales, v_word
         exps(1)
 
         w_t = [shared.tile([P, PAGE], BF16, name="w_t%d" % g, align_bytes=64, offset=WT_AT + (0, 1, 3, 4)[g] * 2 * PAGE) for g in range(PAGES)]
+        w32 = [keep.tile([P, PAGE], F32, name="w32_%d" % g) for g in range(PAGES)]
+        w16 = {g: keep.tile([P, PAGE], BF16, name="w16_%d" % g) for g in range(1, PAGES)}
         for g in range(PAGES):
-            w32 = keep.tile([P, PAGE], F32, name="w32_%d" % g)
-            nc.vector.tensor_tensor(w32[:], vs_win[:].indirect(page_list(g)), p[g][:], ALU.mult)
-            w16 = keep.tile([P, PAGE], BF16, name="w16_%d" % g)
-            nc.scalar.copy(w16[:].rearrange("p (u s e) -> p u s e", u=2, e=2), w32[:].rearrange("p (s u e) -> p u s e", u=2, e=2))
+            nc.vector.tensor_tensor(w32[g][:], vs_win[:].indirect(page_list(g)), p[g][:], ALU.mult)
+        nc.scalar.copy(w16[1][:], w32[1][:])
+        nc.scalar.copy(w16[2][:], w32[2][:])
+        nc.vector.tensor_copy(w16[3][:], w32[3][:])
+        bank = psum.tile([P, 4, NQ], F32, name="bank0", offset=4 * BANK)
+        for t in range(4):
+            nc.tensor.transpose(bank[:, t, :], w32[0][:, t:PAGE:4], ident[:])
+        nc.scalar.copy(w_t[0][:].rearrange("p (q t) -> p q t", t=4), bank[:].rearrange("p t q -> p q t"))
+        for g in range(1, PAGES):
             bank = psum.tile([P, 2, NQ], F32, name="bank%d" % g, offset=(4 + g % 2) * BANK)
             for u in range(2):
-                nc.tensor.transpose(bank[:, u, :], w16[:].bitcast(F32)[:, u * P : (u + 1) * P], ident[:])
+                nc.tensor.transpose(bank[:, u, :], w16[g][:].bitcast(F32)[:, u : PAGE // 2 : 2], ident[:])
             nc.scalar.copy(w_t[g][:].bitcast(F32).rearrange("p (q u) -> p q u", u=2), bank[:].rearrange("p u q -> p q u"))
 
         total = keep.tile([P, B], F32, name="total")
@@ -171,7 +178,7 @@ def tile_attend_pkv4_qpk_kernel(tc, q_words, q_scales, k_words, k_scales, v_word
         v_got.append(gather_values(1, shared.tile([P, 2 * DV], U32, name="v_got1", align_bytes=64, offset=WT_AT + 2 * PAGE)))
         quantise(3)
         for b in range(B):
-            acc = psum.tile([P, DV], F32, name="acc%d" % b, offset=(5 + b) * BANK)
+            acc = psum.tile([P, DV], F32, name="acc%d" % b, offset=(6 + b) * BANK)
             for j in range(2):
                 g = 2 * b + j
                 nc.tensor.matmul_mx(

@@ -24,12 +24,15 @@ ACT = mybir.ActivationFunctionType
 
 V_PLANE = 4
 EDGE = 64
-VS_AT = 0
-KS_TILE_AT = VS_AT + 4 * T - EDGE
-KS_AT = KS_TILE_AT + EDGE
-VW_AT = KS_AT + T
-WT_AT = VW_AT + 4 * POOL_PAGES * DV
+VW_AT = 0
+VSC_AT = VW_AT + 4 * POOL_PAGES * DV - EDGE
+V_PLANE_AT = VSC_AT + 8 * EDGE
+VS_AT = VSC_AT + POOL_PAGES * DV - EDGE
+WT_AT = VS_AT + 4 * T
+KS_AT = WT_AT + 5 * 2 * PAGE
 BANK = 2048
+PIECE = 4096
+VSC_ROW = 64
 
 
 def tile_attend_pkv4_qpk_kernel(tc, q_words, q_scales, k_words, k_scales, v_words, v_scales, vs, offs, voffs, out):
@@ -42,21 +45,21 @@ def tile_attend_pkv4_qpk_kernel(tc, q_words, q_scales, k_words, k_scales, v_word
 
         offs_t = lists.tile([P, B * N // 16], U16, name="offs_t")
         voffs_t = lists.tile([P, PAGES * DV // 16], U16, name="voffs_t")
-        ks_tile = shared.tile([P, (T + 2 * EDGE) // 4], I32, name="ks_tile", align_bytes=64, offset=KS_TILE_AT)
-        ks_win = ks_tile[:, EDGE // 4 : (EDGE + T) // 4]
+        ks_win = shared.tile([P, T // 4], I32, name="ks_win", align_bytes=64, offset=KS_AT)
         kw_win = keep.tile([P, T], I32, name="kw_win")
         q_codes = keep.tile([P, B * PASSES, NQ], I32, name="q_codes", align_bytes=64)
         nc.sync.dma_start(offs_t[:], offs)
         nc.sync.dma_start(ks_win[0:32, :], k_scales.rearrange("o f t -> f o t").bitcast(I32))
         nc.sync.dma_start(voffs_t[:], voffs)
-        nc.sync.dma_start(kw_win[:], k_words[0].rearrange("p t b -> p (t b)").bitcast(I32))
+        nc.sync.dma_start(kw_win[:], k_words[0].rearrange("p t b -> p (t b)").bitcast(I32), max_dma_last_dim=PIECE)
         nc.sync.dma_start(q_codes[:], q_words.rearrange("b o p q t -> p (b o) (q t)").bitcast(I32))
 
-        vsc_win = keep.tile([P, POOL_PAGES * DV // 4], I32, name="vsc_win")
+        vsc_win = shared.tile([P, POOL_PAGES * DV // 4], I32, name="vsc_win", align_bytes=64, offset=VSC_AT)
         nc.vector.memset(vsc_win[:], 0)
-        vsc_rows = v_scales.rearrange("u (g r) e -> r g u e", r=4)
-        for r in range(4):
-            nc.scalar.dma_start(vsc_win[V_PLANE + r : P : 32, :].rearrange("p (u e) -> p u e", u=POOL_PAGES), vsc_rows[r].bitcast(I32))
+        nc.scalar.dma_start(
+            vsc_win[VSC_ROW : VSC_ROW + 16, :].rearrange("p (u e) -> p u e", u=POOL_PAGES),
+            v_scales.rearrange("u f e -> f u e").bitcast(I32),
+        )
 
         q_plane = keep.tile([P, B * PASSES, NQ // 4], I32, name="q_plane", align_bytes=64)
         nc.vector.memset(q_plane[:], 0)
@@ -70,32 +73,39 @@ def tile_attend_pkv4_qpk_kernel(tc, q_words, q_scales, k_words, k_scales, v_word
         make_identity(nc, ident[:])
 
         ks_got = keep.tile([P, B * N], U8, name="ks_got")
-        nc.vector.tensor_copy(ks_got[:], ks_win.bitcast(U8).indirect(offs_t[:]))
+        nc.vector.tensor_copy(ks_got[:], ks_win[:].bitcast(U8).indirect(offs_t[:]))
         k_plane = shared.tile([P, PASSES, B * N // 4], I32, name="k_plane", align_bytes=64, offset=KS_AT)
         for quad in (0, 2, 1, 3):
             nc.sync.dma_start(k_plane[32 * quad : 32 * quad + 4, :, :], ks_got[8 * quad : 8 * quad + 8, :].bitcast(I32))
+
+        vsc_got = keep.tile([P, PAGES * DV], U8, name="vsc_got")
+        nc.vector.tensor_copy(vsc_got[:], vsc_win[:].bitcast(U8).indirect(voffs_t[:]))
         vs_win = shared.tile([P, T], F32, name="vs_win", align_bytes=64, offset=VS_AT)
-        nc.sync.dma_start(vs_win[:], vs)
+        nc.sync.dma_start(vs_win[:], vs, max_dma_last_dim=PIECE)
         vw_win = shared.tile([P, POOL_PAGES * DV], I32, name="vw_win", align_bytes=64, offset=VW_AT)
         nc.sync.dma_start(
             vw_win[:].rearrange("p (u e) -> p u e", u=POOL_PAGES),
             v_words.rearrange("u p e r -> p u (e r)").bitcast(I32),
         )
-
-        v_plane = keep.tile([P, PAGES * DV], U8, name="v_plane", align_bytes=64)
-        nc.vector.tensor_copy(v_plane[:], vsc_win[:].bitcast(U8).indirect(voffs_t[:]))
+        v_plane = shared.tile([P, PAGES * DV // 4], I32, name="v_plane", align_bytes=64, offset=V_PLANE_AT)
+        for quad in range(4):
+            nc.sync.dma_start(
+                v_plane[32 * quad + V_PLANE : 32 * quad + V_PLANE + 4, :],
+                vsc_got[VSC_ROW + 4 * quad : VSC_ROW + 4 * quad + 4, :].bitcast(I32),
+            )
 
         def page_list(g):
             return offs_t[:, g * PAGE // 16 : (g + 1) * PAGE // 16]
 
         scores = [psum.tile([P, PAGE], F32, name="scores%d" % g, offset=g * BANK) for g in range(PAGES)]
-        k_got = [keep.tile([P, PAGE], U32, name="k_got%d" % g) for g in range(PAGES)]
+        k_got = {}
         neg_score = [keep.tile([P, PAGE], F32, name="neg_score%d" % g) for g in range(PAGES)]
         neg_max = [keep.tile([P, 1], F32, name="neg_max%d" % g) for g in range(PAGES)]
         p = [keep.tile([P, PAGE], F32, name="p%d" % g, tag="p%d" % g, align_bytes=64) for g in range(PAGES)]
         sums = keep.tile([P, 2, B], F32, name="sums")
 
         def gather_keys(g):
+            k_got[g] = keep.tile([P, PAGE], U32, name="k_got%d" % g, tag="k_got%d" % (g % 2))
             nc.vector.tensor_copy(k_got[g][:], kw_win[:].bitcast(U32).indirect(page_list(g)))
 
         def score(g):
@@ -127,8 +137,8 @@ def tile_attend_pkv4_qpk_kernel(tc, q_words, q_scales, k_words, k_scales, v_word
         gather_keys(0)
         gather_keys(1)
         score(0)
-        gather_keys(2)
         score(1)
+        gather_keys(2)
         gather_keys(3)
         score(2)
         row_max(0)
@@ -186,7 +196,7 @@ def tile_attend_pkv4_qpk_kernel(tc, q_words, q_scales, k_words, k_scales, v_word
                     lhsT=w_codes[g][:].bitcast(FP8X4),
                     lhsT_scale=w_plane[g][:],
                     rhs=v_got[b][:, j * DV : (j + 1) * DV].bitcast(FP8X4),
-                    rhs_scale=v_plane[V_PLANE:P, g * DV : (g + 1) * DV],
+                    rhs_scale=v_plane[V_PLANE:P, g * DV // 4 : (g + 1) * DV // 4].bitcast(U8),
                     start=(j == 0),
                     stop=(j == 1),
                 )

@@ -52,7 +52,6 @@ def tile_attend_pkv4_qpk_kernel(tc, q_words, q_scales, k_words, k_scales, v_word
         nc.sync.dma_start(ks_win[0:32, :], k_scales.rearrange("o f t -> f o t").bitcast(I32))
         nc.sync.dma_start(voffs_t[:], voffs)
         nc.sync.dma_start(kw_win[:], k_words[0].rearrange("p t b -> p (t b)").bitcast(I32), max_dma_last_dim=PIECE)
-        nc.sync.dma_start(q_codes[:], q_words.rearrange("b o p q t -> p (b o) (q t)").bitcast(I32))
 
         vsc_win = shared.tile([P, POOL_PAGES * DV // 4], I32, name="vsc_win", align_bytes=64, offset=VSC_AT)
         nc.vector.memset(vsc_win[:], 0)
@@ -65,7 +64,8 @@ def tile_attend_pkv4_qpk_kernel(tc, q_words, q_scales, k_words, k_scales, v_word
         nc.vector.memset(q_plane[:], 0)
         qs_rows = q_scales.rearrange("b o (g r) q -> r g (b o) q", r=4)
         for r in range(4):
-            nc.scalar.dma_start(q_plane[r:P:32, :, :], qs_rows[r].bitcast(I32))
+            nc.sync.dma_start(q_plane[r:P:32, :, :], qs_rows[r].bitcast(I32))
+        nc.sync.dma_start(q_codes[:], q_words.rearrange("b o p q t -> p (b o) (q t)").bitcast(I32))
 
         nc.vector.memset(ks_win[32:64, :], 0)
         nc.gpsimd.memset(ks_win[64:128, :], 0)
@@ -99,10 +99,13 @@ def tile_attend_pkv4_qpk_kernel(tc, q_words, q_scales, k_words, k_scales, v_word
 
         scores = [psum.tile([P, PAGE], F32, name="scores%d" % g, offset=g * BANK) for g in range(PAGES)]
         k_got = {}
-        neg_score = [keep.tile([P, PAGE], F32, name="neg_score%d" % g) for g in range(PAGES)]
+        neg_score = [keep.tile([P, N], F32, name="neg_score%d" % b) for b in range(B)]
         neg_max = [keep.tile([P, 1], F32, name="neg_max%d" % g) for g in range(PAGES)]
-        p = [keep.tile([P, PAGE], F32, name="p%d" % g, tag="p%d" % g, align_bytes=64) for g in range(PAGES)]
-        sums = keep.tile([P, 2, B], F32, name="sums")
+        p = [keep.tile([P, N], F32, name="p%d" % b, tag="p%d" % b, align_bytes=64) for b in range(B)]
+        total = keep.tile([P, B], F32, name="total")
+
+        def page_of(tiles, g):
+            return tiles[g // 2][:, (g % 2) * PAGE : (g % 2 + 1) * PAGE]
 
         def gather_keys(g):
             k_got[g] = keep.tile([P, PAGE], U32, name="k_got%d" % g, tag="k_got%d" % (g % 2))
@@ -125,14 +128,12 @@ def tile_attend_pkv4_qpk_kernel(tc, q_words, q_scales, k_words, k_scales, v_word
 
         def row_max(g):
             nc.vector.tensor_scalar(
-                neg_score[g][:], scores[g][:], -1.0, neg_max[g - 1][:] if g % 2 else None,
+                page_of(neg_score, g), scores[g][:], -1.0, neg_max[g - 1][:] if g % 2 else None,
                 ALU.mult, ALU.min, accum_out=neg_max[g][:],
             )
 
         def exps(b):
-            for j in range(2):
-                g = 2 * b + j
-                nc.scalar.activation(p[g][:], neg_score[g][:], ACT.Exp, bias=neg_max[2 * b + 1][:], scale=-1.0, accum_out=sums[:, j, b : b + 1])
+            nc.scalar.activation(p[b][:], neg_score[b][:], ACT.Exp, bias=neg_max[2 * b + 1][:], scale=-1.0, accum_out=total[:, b : b + 1])
 
         gather_keys(0)
         gather_keys(1)
@@ -149,27 +150,36 @@ def tile_attend_pkv4_qpk_kernel(tc, q_words, q_scales, k_words, k_scales, v_word
         row_max(3)
         exps(1)
 
-        w_t = [shared.tile([P, PAGE], BF16, name="w_t%d" % g, align_bytes=64, offset=WT_AT + (0, 1, 3, 4)[g] * 2 * PAGE) for g in range(PAGES)]
+        w_t = [shared.tile([P, PAGE], BF16, name="w_t%d" % g, align_bytes=64, offset=WT_AT + (0, 2, 3, 4)[g] * 2 * PAGE) for g in range(PAGES)]
         w32 = [keep.tile([P, PAGE], F32, name="w32_%d" % g) for g in range(PAGES)]
         w16 = {g: keep.tile([P, PAGE], BF16, name="w16_%d" % g) for g in range(1, PAGES)}
         for g in range(PAGES):
-            nc.vector.tensor_tensor(w32[g][:], vs_win[:].indirect(page_list(g)), p[g][:], ALU.mult)
-        nc.scalar.copy(w16[1][:], w32[1][:])
-        nc.scalar.copy(w16[2][:], w32[2][:])
-        nc.vector.tensor_copy(w16[3][:], w32[3][:])
-        bank = psum.tile([P, 4, NQ], F32, name="bank0", offset=4 * BANK)
-        for t in range(4):
-            nc.tensor.transpose(bank[:, t, :], w32[0][:, t:PAGE:4], ident[:])
-        nc.scalar.copy(w_t[0][:].rearrange("p (q t) -> p q t", t=4), bank[:].rearrange("p t q -> p q t"))
-        for g in range(1, PAGES):
+            nc.vector.tensor_tensor(w32[g][:], vs_win[:].indirect(page_list(g)), page_of(p, g), ALU.mult)
+
+        def round_page(g):
+            nc.scalar.copy(w16[g][:].rearrange("p (u s e) -> p u s e", u=2, e=2), w32[g][:].rearrange("p (s u e) -> p u s e", u=2, e=2))
+
+        def turn_first_page():
+            bank = psum.tile([P, 4, NQ], F32, name="bank0", offset=4 * BANK)
+            for t in range(4):
+                nc.tensor.transpose(bank[:, t, :], w32[0][:, t:PAGE:4], ident[:])
+            nc.scalar.copy(w_t[0][:].rearrange("p (q t) -> p q t", t=4), bank[:].rearrange("p t q -> p q t"))
+
+        def turn_pairs(g):
             bank = psum.tile([P, 2, NQ], F32, name="bank%d" % g, offset=(4 + g % 2) * BANK)
             for u in range(2):
-                nc.tensor.transpose(bank[:, u, :], w16[g][:].bitcast(F32)[:, u : PAGE // 2 : 2], ident[:])
+                nc.tensor.transpose(bank[:, u, :], w16[g][:].bitcast(F32)[:, u * P : (u + 1) * P], ident[:])
             nc.scalar.copy(w_t[g][:].bitcast(F32).rearrange("p (q u) -> p q u", u=2), bank[:].rearrange("p u q -> p q u"))
 
-        total = keep.tile([P, B], F32, name="total")
+        round_page(1)
+        turn_first_page()
+        round_page(2)
+        turn_pairs(1)
+        round_page(3)
+        turn_pairs(2)
+        turn_pairs(3)
+
         inv = keep.tile([P, B], F32, name="inv")
-        nc.vector.tensor_tensor(total[:], sums[:, 0, :], sums[:, 1, :], ALU.add)
         w_codes = [keep.tile([P, NQ], U32, name="w_codes%d" % g, align_bytes=64) for g in range(PAGES)]
         w_plane = [keep.tile([P, NQ], U8, name="w_plane%d" % g, align_bytes=64) for g in range(PAGES)]
 
@@ -180,29 +190,36 @@ def tile_attend_pkv4_qpk_kernel(tc, q_words, q_scales, k_words, k_scales, v_word
             nc.vector.tensor_copy(got[:], vw_win[:].bitcast(U32).indirect(voffs_t[:, b * 32 : (b + 1) * 32]))
             return got
 
-        v_got = [gather_values(0, keep.tile([P, 2 * DV], U32, name="v_got0", tag="p2", align_bytes=64))]
+        v_got = [gather_values(0, keep.tile([P, 2 * DV], U32, name="v_got0", tag="p0", align_bytes=64))]
         quantise(0)
         nc.vector.reciprocal(inv[:], total[:])
         quantise(1)
+        v_got.append(gather_values(1, shared.tile([P, 2 * DV], U32, name="v_got1", align_bytes=64, offset=WT_AT)))
         quantise(2)
-        v_got.append(gather_values(1, shared.tile([P, 2 * DV], U32, name="v_got1", align_bytes=64, offset=WT_AT + 2 * PAGE)))
         quantise(3)
-        for b in range(B):
-            acc = psum.tile([P, DV], F32, name="acc%d" % b, offset=(6 + b) * BANK)
+
+        def product(b, bank, cols):
+            acc = psum.tile([P, cols.stop - cols.start], F32, name="acc%d" % bank, offset=bank * BANK)
             for j in range(2):
                 g = 2 * b + j
                 nc.tensor.matmul_mx(
                     out=acc[:],
                     lhsT=w_codes[g][:].bitcast(FP8X4),
                     lhsT_scale=w_plane[g][:],
-                    rhs=v_got[b][:, j * DV : (j + 1) * DV].bitcast(FP8X4),
-                    rhs_scale=v_plane[V_PLANE:P, g * DV // 4 : (g + 1) * DV // 4].bitcast(U8),
+                    rhs=v_got[b][:, j * DV + cols.start : j * DV + cols.stop].bitcast(FP8X4),
+                    rhs_scale=v_plane[V_PLANE:P, (g * DV + cols.start) // 4 : (g * DV + cols.stop) // 4].bitcast(U8),
                     start=(j == 0),
                     stop=(j == 1),
                 )
-            y = keep.tile([P, DV], F32, name="y%d" % b)
-            if b == 0:
-                nc.scalar.activation(y[:], acc[:], ACT.Copy, scale=inv[:, b : b + 1])
-            else:
-                nc.vector.tensor_scalar(y[:], acc[:], inv[:, b : b + 1], None, ALU.mult)
-            nc.sync.dma_start(out[b], y[:])
+            return acc
+
+        whole, low, high = slice(0, DV), slice(0, DV // 2), slice(DV // 2, DV)
+        y0 = keep.tile([P, DV], F32, name="y0")
+        nc.scalar.activation(y0[:], product(0, 6, whole)[:], ACT.Copy, scale=inv[:, 0:1])
+        nc.sync.dma_start(out[0], y0[:])
+        y_low = keep.tile([P, DV // 2], F32, name="y_low")
+        nc.vector.tensor_scalar(y_low[:], product(1, 7, low)[:], inv[:, 1:2], None, ALU.mult)
+        nc.sync.dma_start(out[1][:, low], y_low[:])
+        y_high = keep.tile([P, DV // 2], F32, name="y_high")
+        nc.scalar.activation(y_high[:], product(1, 0, high)[:], ACT.Copy, scale=inv[:, 1:2])
+        nc.scalar.dma_start(out[1][:, high], y_high[:])

@@ -51,7 +51,10 @@ def tile_attend_pkv4_qpk_kernel(tc, q_words, q_scales, k_words, k_scales, v_word
         nc.sync.dma_start(offs_t[:], offs)
         nc.sync.dma_start(ks_win[0:32, :], k_scales.rearrange("o f t -> f o t").bitcast(I32))
         nc.sync.dma_start(voffs_t[:], voffs)
-        nc.sync.dma_start(kw_win[:], k_words[0].rearrange("p t b -> p (t b)").bitcast(I32), max_dma_last_dim=PIECE)
+        kw_rows = k_words[0].rearrange("p t b -> p (t b)").bitcast(I32)
+        for half in (slice(0, T // 2), slice(T // 2, T)):
+            nc.sync.dma_start(kw_win[:, half], kw_rows[:, half], max_dma_last_dim=PIECE)
+        nc.sync.dma_start(q_codes[:], q_words.rearrange("b o p q t -> p (b o) (q t)").bitcast(I32))
 
         vsc_win = shared.tile([P, POOL_PAGES * DV // 4], I32, name="vsc_win", align_bytes=64, offset=VSC_AT)
         nc.vector.memset(vsc_win[:], 0)
@@ -64,8 +67,7 @@ def tile_attend_pkv4_qpk_kernel(tc, q_words, q_scales, k_words, k_scales, v_word
         nc.vector.memset(q_plane[:], 0)
         qs_rows = q_scales.rearrange("b o (g r) q -> r g (b o) q", r=4)
         for r in range(4):
-            nc.sync.dma_start(q_plane[r:P:32, :, :], qs_rows[r].bitcast(I32))
-        nc.sync.dma_start(q_codes[:], q_words.rearrange("b o p q t -> p (b o) (q t)").bitcast(I32))
+            nc.scalar.dma_start(q_plane[r:P:32, :, :], qs_rows[r].bitcast(I32))
 
         nc.vector.memset(ks_win[32:64, :], 0)
         nc.gpsimd.memset(ks_win[64:128, :], 0)

@@ -24,12 +24,11 @@ ACT = mybir.ActivationFunctionType
 
 V_PLANE = 4
 EDGE = 64
-VW_AT = 0
-VSC_AT = VW_AT + 4 * POOL_PAGES * DV - EDGE
-V_PLANE_AT = VSC_AT + 8 * EDGE
-VS_AT = VSC_AT + POOL_PAGES * DV - EDGE
-WT_AT = VS_AT + 4 * T
-KS_AT = WT_AT + 5 * 2 * PAGE
+VS_AT = 0
+KS_AT = VS_AT + 4 * T
+VW_AT = KS_AT + T
+WT_AT = VW_AT + 4 * POOL_PAGES * DV
+VSC_AT = WT_AT + 5 * 2 * PAGE
 BANK = 2048
 PIECE = 4096
 VSC_ROW = 64
@@ -45,7 +44,8 @@ def tile_attend_pkv4_qpk_kernel(tc, q_words, q_scales, k_words, k_scales, v_word
 
         offs_t = lists.tile([P, B * N // 16], U16, name="offs_t")
         voffs_t = lists.tile([P, PAGES * DV // 16], U16, name="voffs_t")
-        ks_win = shared.tile([P, T // 4], I32, name="ks_win", align_bytes=64, offset=KS_AT)
+        ks_tile = shared.tile([P, (T + 2 * EDGE) // 4], I32, name="ks_tile", align_bytes=64, offset=KS_AT - EDGE)
+        ks_win = ks_tile[:, EDGE // 4 : (EDGE + T) // 4]
         kw_win = keep.tile([P, T], I32, name="kw_win")
         q_codes = keep.tile([P, B * PASSES, NQ], I32, name="q_codes", align_bytes=64)
         nc.sync.dma_start(offs_t[:], offs)
@@ -75,7 +75,7 @@ def tile_attend_pkv4_qpk_kernel(tc, q_words, q_scales, k_words, k_scales, v_word
         make_identity(nc, ident[:])
 
         ks_got = keep.tile([P, B * N], U8, name="ks_got")
-        nc.vector.tensor_copy(ks_got[:], ks_win[:].bitcast(U8).indirect(offs_t[:]))
+        nc.vector.tensor_copy(ks_got[:], ks_win.bitcast(U8).indirect(offs_t[:]))
         k_plane = shared.tile([P, PASSES, B * N // 4], I32, name="k_plane", align_bytes=64, offset=KS_AT)
         for quad in (0, 2, 1, 3):
             nc.sync.dma_start(k_plane[32 * quad : 32 * quad + 4, :, :], ks_got[8 * quad : 8 * quad + 8, :].bitcast(I32))
@@ -89,7 +89,7 @@ def tile_attend_pkv4_qpk_kernel(tc, q_words, q_scales, k_words, k_scales, v_word
             vw_win[:].rearrange("p (u e) -> p u e", u=POOL_PAGES),
             v_words.rearrange("u p e r -> p u (e r)").bitcast(I32),
         )
-        v_plane = shared.tile([P, PAGES * DV // 4], I32, name="v_plane", align_bytes=64, offset=V_PLANE_AT)
+        v_plane = shared.tile([P, PAGES * DV // 4], I32, name="v_plane", align_bytes=64, offset=VSC_AT)
         for quad in range(4):
             nc.sync.dma_start(
                 v_plane[32 * quad + V_PLANE : 32 * quad + V_PLANE + 4, :],
@@ -101,13 +101,10 @@ def tile_attend_pkv4_qpk_kernel(tc, q_words, q_scales, k_words, k_scales, v_word
 
         scores = [psum.tile([P, PAGE], F32, name="scores%d" % g, offset=g * BANK) for g in range(PAGES)]
         k_got = {}
-        neg_score = [keep.tile([P, N], F32, name="neg_score%d" % b) for b in range(B)]
+        neg_score = [keep.tile([P, PAGE], F32, name="neg_score%d" % g) for g in range(PAGES)]
         neg_max = [keep.tile([P, 1], F32, name="neg_max%d" % g) for g in range(PAGES)]
-        p = [keep.tile([P, N], F32, name="p%d" % b, tag="p%d" % b, align_bytes=64) for b in range(B)]
-        total = keep.tile([P, B], F32, name="total")
-
-        def page_of(tiles, g):
-            return tiles[g // 2][:, (g % 2) * PAGE : (g % 2 + 1) * PAGE]
+        p = [keep.tile([P, PAGE], F32, name="p%d" % g, tag="p%d" % g, align_bytes=64) for g in range(PAGES)]
+        sums = keep.tile([P, 2, B], F32, name="sums")
 
         def gather_keys(g):
             k_got[g] = keep.tile([P, PAGE], U32, name="k_got%d" % g, tag="k_got%d" % (g % 2))
@@ -130,12 +127,14 @@ def tile_attend_pkv4_qpk_kernel(tc, q_words, q_scales, k_words, k_scales, v_word
 
         def row_max(g):
             nc.vector.tensor_scalar(
-                page_of(neg_score, g), scores[g][:], -1.0, neg_max[g - 1][:] if g % 2 else None,
+                neg_score[g][:], scores[g][:], -1.0, neg_max[g - 1][:] if g % 2 else None,
                 ALU.mult, ALU.min, accum_out=neg_max[g][:],
             )
 
         def exps(b):
-            nc.scalar.activation(p[b][:], neg_score[b][:], ACT.Exp, bias=neg_max[2 * b + 1][:], scale=-1.0, accum_out=total[:, b : b + 1])
+            for j in range(2):
+                g = 2 * b + j
+                nc.scalar.activation(p[g][:], neg_score[g][:], ACT.Exp, bias=neg_max[2 * b + 1][:], scale=-1.0, accum_out=sums[:, j, b : b + 1])
 
         gather_keys(0)
         gather_keys(1)
@@ -152,36 +151,27 @@ def tile_attend_pkv4_qpk_kernel(tc, q_words, q_scales, k_words, k_scales, v_word
         row_max(3)
         exps(1)
 
-        w_t = [shared.tile([P, PAGE], BF16, name="w_t%d" % g, align_bytes=64, offset=WT_AT + (0, 2, 3, 4)[g] * 2 * PAGE) for g in range(PAGES)]
+        w_t = [shared.tile([P, PAGE], BF16, name="w_t%d" % g, align_bytes=64, offset=WT_AT + (0, 1, 3, 4)[g] * 2 * PAGE) for g in range(PAGES)]
         w32 = [keep.tile([P, PAGE], F32, name="w32_%d" % g) for g in range(PAGES)]
         w16 = {g: keep.tile([P, PAGE], BF16, name="w16_%d" % g) for g in range(1, PAGES)}
         for g in range(PAGES):
-            nc.vector.tensor_tensor(w32[g][:], vs_win[:].indirect(page_list(g)), page_of(p, g), ALU.mult)
-
-        def round_page(g):
-            nc.scalar.copy(w16[g][:].rearrange("p (u s e) -> p u s e", u=2, e=2), w32[g][:].rearrange("p (s u e) -> p u s e", u=2, e=2))
-
-        def turn_first_page():
-            bank = psum.tile([P, 4, NQ], F32, name="bank0", offset=4 * BANK)
-            for t in range(4):
-                nc.tensor.transpose(bank[:, t, :], w32[0][:, t:PAGE:4], ident[:])
-            nc.scalar.copy(w_t[0][:].rearrange("p (q t) -> p q t", t=4), bank[:].rearrange("p t q -> p q t"))
-
-        def turn_pairs(g):
+            nc.vector.tensor_tensor(w32[g][:], vs_win[:].indirect(page_list(g)), p[g][:], ALU.mult)
+        nc.scalar.copy(w16[1][:], w32[1][:])
+        nc.scalar.copy(w16[2][:], w32[2][:])
+        nc.vector.tensor_copy(w16[3][:], w32[3][:])
+        bank = psum.tile([P, 4, NQ], F32, name="bank0", offset=4 * BANK)
+        for t in range(4):
+            nc.tensor.transpose(bank[:, t, :], w32[0][:, t:PAGE:4], ident[:])
+        nc.scalar.copy(w_t[0][:].rearrange("p (q t) -> p q t", t=4), bank[:].rearrange("p t q -> p q t"))
+        for g in range(1, PAGES):
             bank = psum.tile([P, 2, NQ], F32, name="bank%d" % g, offset=(4 + g % 2) * BANK)
             for u in range(2):
-                nc.tensor.transpose(bank[:, u, :], w16[g][:].bitcast(F32)[:, u * P : (u + 1) * P], ident[:])
+                nc.tensor.transpose(bank[:, u, :], w16[g][:].bitcast(F32)[:, u : PAGE // 2 : 2], ident[:])
             nc.scalar.copy(w_t[g][:].bitcast(F32).rearrange("p (q u) -> p q u", u=2), bank[:].rearrange("p u q -> p q u"))
 
-        round_page(1)
-        turn_first_page()
-        round_page(2)
-        turn_pairs(1)
-        round_page(3)
-        turn_pairs(2)
-        turn_pairs(3)
-
+        total = keep.tile([P, B], F32, name="total")
         inv = keep.tile([P, B], F32, name="inv")
+        nc.vector.tensor_tensor(total[:], sums[:, 0, :], sums[:, 1, :], ALU.add)
         w_codes = [keep.tile([P, NQ], U32, name="w_codes%d" % g, align_bytes=64) for g in range(PAGES)]
         w_plane = [keep.tile([P, NQ], U8, name="w_plane%d" % g, align_bytes=64) for g in range(PAGES)]
 
@@ -192,36 +182,29 @@ def tile_attend_pkv4_qpk_kernel(tc, q_words, q_scales, k_words, k_scales, v_word
             nc.vector.tensor_copy(got[:], vw_win[:].bitcast(U32).indirect(voffs_t[:, b * 32 : (b + 1) * 32]))
             return got
 
-        v_got = [gather_values(0, keep.tile([P, 2 * DV], U32, name="v_got0", tag="p0", align_bytes=64))]
+        v_got = [gather_values(0, keep.tile([P, 2 * DV], U32, name="v_got0", tag="p2", align_bytes=64))]
         quantise(0)
         nc.vector.reciprocal(inv[:], total[:])
         quantise(1)
-        v_got.append(gather_values(1, shared.tile([P, 2 * DV], U32, name="v_got1", align_bytes=64, offset=WT_AT)))
         quantise(2)
+        v_got.append(gather_values(1, shared.tile([P, 2 * DV], U32, name="v_got1", align_bytes=64, offset=WT_AT + 2 * PAGE)))
         quantise(3)
-
-        def product(b, bank, cols):
-            acc = psum.tile([P, cols.stop - cols.start], F32, name="acc%d" % bank, offset=bank * BANK)
+        for b in range(B):
+            acc = psum.tile([P, DV], F32, name="acc%d" % b, offset=(6 + b) * BANK)
             for j in range(2):
                 g = 2 * b + j
                 nc.tensor.matmul_mx(
                     out=acc[:],
                     lhsT=w_codes[g][:].bitcast(FP8X4),
                     lhsT_scale=w_plane[g][:],
-                    rhs=v_got[b][:, j * DV + cols.start : j * DV + cols.stop].bitcast(FP8X4),
-                    rhs_scale=v_plane[V_PLANE:P, (g * DV + cols.start) // 4 : (g * DV + cols.stop) // 4].bitcast(U8),
+                    rhs=v_got[b][:, j * DV : (j + 1) * DV].bitcast(FP8X4),
+                    rhs_scale=v_plane[V_PLANE:P, g * DV // 4 : (g + 1) * DV // 4].bitcast(U8),
                     start=(j == 0),
                     stop=(j == 1),
                 )
-            return acc
-
-        whole, low, high = slice(0, DV), slice(0, DV // 2), slice(DV // 2, DV)
-        y0 = keep.tile([P, DV], F32, name="y0")
-        nc.scalar.activation(y0[:], product(0, 6, whole)[:], ACT.Copy, scale=inv[:, 0:1])
-        nc.sync.dma_start(out[0], y0[:])
-        y_low = keep.tile([P, DV // 2], F32, name="y_low")
-        nc.vector.tensor_scalar(y_low[:], product(1, 7, low)[:], inv[:, 1:2], None, ALU.mult)
-        nc.sync.dma_start(out[1][:, low], y_low[:])
-        y_high = keep.tile([P, DV // 2], F32, name="y_high")
-        nc.scalar.activation(y_high[:], product(1, 0, high)[:], ACT.Copy, scale=inv[:, 1:2])
-        nc.scalar.dma_start(out[1][:, high], y_high[:])
+            y = keep.tile([P, DV], F32, name="y%d" % b)
+            if b == 0:
+                nc.scalar.activation(y[:], acc[:], ACT.Copy, scale=inv[:, b : b + 1])
+            else:
+                nc.vector.tensor_scalar(y[:], acc[:], inv[:, b : b + 1], None, ALU.mult)
+            nc.sync.dma_start(out[b], y[:])

@@ -31,7 +31,8 @@ WT_AT = VW_AT + 4 * POOL_PAGES * DV
 VSC_AT = WT_AT + 5 * 2 * PAGE
 BANK = 2048
 PIECE = 4096
-VSC_ROW = 64
+VSC_ROW = 16
+KS_ROW = 96
 
 
 def tile_attend_pkv4_qpk_kernel(tc, q_words, q_scales, k_words, k_scales, v_words, v_scales, vs, offs, voffs, out):
@@ -49,16 +50,16 @@ def tile_attend_pkv4_qpk_kernel(tc, q_words, q_scales, k_words, k_scales, v_word
         kw_win = keep.tile([P, T], I32, name="kw_win")
         q_codes = keep.tile([P, B * PASSES, NQ], I32, name="q_codes", align_bytes=64)
         nc.sync.dma_start(offs_t[:], offs)
-        nc.sync.dma_start(ks_win[0:32, :], k_scales.rearrange("o f t -> f o t").bitcast(I32))
+        nc.scalar.dma_start(ks_win[KS_ROW:P, :], k_scales.rearrange("o f t -> f o t").bitcast(I32))
         nc.sync.dma_start(voffs_t[:], voffs)
         kw_rows = k_words[0].rearrange("p t b -> p (t b)").bitcast(I32)
         for half in (slice(0, T // 2), slice(T // 2, T)):
-            nc.sync.dma_start(kw_win[:, half], kw_rows[:, half], max_dma_last_dim=PIECE)
-        nc.sync.dma_start(q_codes[:], q_words.rearrange("b o p q t -> p (b o) (q t)").bitcast(I32))
+            nc.scalar.dma_start(kw_win[:, half], kw_rows[:, half], max_dma_last_dim=PIECE)
+        nc.scalar.dma_start(q_codes[:], q_words.rearrange("b o p q t -> p (b o) (q t)").bitcast(I32))
 
         vsc_win = shared.tile([P, POOL_PAGES * DV // 4], I32, name="vsc_win", align_bytes=64, offset=VSC_AT)
         nc.vector.memset(vsc_win[:], 0)
-        nc.scalar.dma_start(
+        nc.sync.dma_start(
             vsc_win[VSC_ROW : VSC_ROW + 16, :].rearrange("p (u e) -> p u e", u=POOL_PAGES),
             v_scales.rearrange("u f e -> f u e").bitcast(I32),
         )
@@ -67,10 +68,9 @@ def tile_attend_pkv4_qpk_kernel(tc, q_words, q_scales, k_words, k_scales, v_word
         nc.vector.memset(q_plane[:], 0)
         qs_rows = q_scales.rearrange("b o (g r) q -> r g (b o) q", r=4)
         for r in range(4):
-            nc.scalar.dma_start(q_plane[r:P:32, :, :], qs_rows[r].bitcast(I32))
+            nc.sync.dma_start(q_plane[r:P:32, :, :], qs_rows[r].bitcast(I32))
 
-        nc.vector.memset(ks_win[32:64, :], 0)
-        nc.gpsimd.memset(ks_win[64:128, :], 0)
+        nc.vector.memset(ks_win[0:KS_ROW, :], 0)
         ident = keep.tile([P, P], F32, name="ident")
         make_identity(nc, ident[:])
 
@@ -78,7 +78,7 @@ def tile_attend_pkv4_qpk_kernel(tc, q_words, q_scales, k_words, k_scales, v_word
         nc.vector.tensor_copy(ks_got[:], ks_win.bitcast(U8).indirect(offs_t[:]))
         k_plane = shared.tile([P, PASSES, B * N // 4], I32, name="k_plane", align_bytes=64, offset=KS_AT)
         for quad in (0, 2, 1, 3):
-            nc.sync.dma_start(k_plane[32 * quad : 32 * quad + 4, :, :], ks_got[8 * quad : 8 * quad + 8, :].bitcast(I32))
+            nc.sync.dma_start(k_plane[32 * quad : 32 * quad + 4, :, :], ks_got[KS_ROW + 8 * quad : KS_ROW + 8 * quad + 8, :].bitcast(I32))
 
         vsc_got = keep.tile([P, PAGES * DV], U8, name="vsc_got")
         nc.vector.tensor_copy(vsc_got[:], vsc_win[:].bitcast(U8).indirect(voffs_t[:]))

@@ -26,13 +26,15 @@ V_PLANE = 4
 EDGE = 64
 VS_AT = 0
 KS_AT = VS_AT + 4 * T
-VW_AT = KS_AT + T
+VP_AT = KS_AT + T
+VW_AT = VP_AT + PAGES * DV
 WT_AT = VW_AT + 4 * POOL_PAGES * DV
 VSC_AT = WT_AT + 5 * 2 * PAGE
 BANK = 2048
 PIECE = 4096
-VSC_ROW = 16
-KS_ROW = 96
+VSC_ROW = 112
+KS_STEP = 4
+KW_FIRST = PIECE // 4
 
 
 def tile_attend_pkv4_qpk_kernel(tc, q_words, q_scales, k_words, k_scales, v_words, v_scales, vs, offs, voffs, out):
@@ -45,32 +47,36 @@ def tile_attend_pkv4_qpk_kernel(tc, q_words, q_scales, k_words, k_scales, v_word
 
         offs_t = lists.tile([P, B * N // 16], U16, name="offs_t")
         voffs_t = lists.tile([P, PAGES * DV // 16], U16, name="voffs_t")
-        ks_tile = shared.tile([P, (T + 2 * EDGE) // 4], I32, name="ks_tile", align_bytes=64, offset=KS_AT - EDGE)
+        ks_tile = shared.tile([P, (VW_AT - KS_AT + 2 * EDGE) // 4], I32, name="ks_tile", align_bytes=64, offset=KS_AT - EDGE)
         ks_win = ks_tile[:, EDGE // 4 : (EDGE + T) // 4]
+        vsc_win = shared.tile([P, POOL_PAGES * DV // 4], I32, name="vsc_win", align_bytes=64, offset=VSC_AT)
         kw_win = keep.tile([P, T], I32, name="kw_win")
         q_codes = keep.tile([P, B * PASSES, NQ], I32, name="q_codes", align_bytes=64)
-        nc.sync.dma_start(offs_t[:], offs)
-        nc.scalar.dma_start(ks_win[KS_ROW:P, :], k_scales.rearrange("o f t -> f o t").bitcast(I32))
-        nc.sync.dma_start(voffs_t[:], voffs)
-        kw_rows = k_words[0].rearrange("p t b -> p (t b)").bitcast(I32)
-        for half in (slice(0, T // 2), slice(T // 2, T)):
-            nc.scalar.dma_start(kw_win[:, half], kw_rows[:, half], max_dma_last_dim=PIECE)
-        nc.scalar.dma_start(q_codes[:], q_words.rearrange("b o p q t -> p (b o) (q t)").bitcast(I32))
-
-        vsc_win = shared.tile([P, POOL_PAGES * DV // 4], I32, name="vsc_win", align_bytes=64, offset=VSC_AT)
-        nc.vector.memset(vsc_win[:], 0)
-        nc.sync.dma_start(
-            vsc_win[VSC_ROW : VSC_ROW + 16, :].rearrange("p (u e) -> p u e", u=POOL_PAGES),
-            v_scales.rearrange("u f e -> f u e").bitcast(I32),
-        )
-
         q_plane = keep.tile([P, B * PASSES, NQ // 4], I32, name="q_plane", align_bytes=64)
         nc.vector.memset(q_plane[:], 0)
+        nc.gpsimd.memset(ks_win, 0)
+        nc.vector.memset(vsc_win[0:VSC_ROW, :], 0)
+        nc.vector.memset(ks_tile[:, (EDGE + T) // 4 : (EDGE + VW_AT - KS_AT) // 4], 0)
+
+        nc.sync.dma_start(voffs_t[:], voffs)
+        nc.scalar.dma_start(
+            vsc_win[VSC_ROW:P, :].rearrange("p (u e) -> p u e", u=POOL_PAGES),
+            v_scales.rearrange("u f e -> f u e").bitcast(I32),
+        )
+        nc.sync.dma_start(offs_t[:], offs)
+        kw_rows = k_words[0].rearrange("p t b -> p (t b)").bitcast(I32)
+        nc.scalar.dma_start(kw_win[:, 0:KW_FIRST], kw_rows[:, 0:KW_FIRST])
+        nc.scalar.dma_start(ks_win[0:P:KS_STEP, :], k_scales.rearrange("o f t -> f o t").bitcast(I32))
+        nc.scalar.dma_start(kw_win[:, KW_FIRST:T], kw_rows[:, KW_FIRST:T], max_dma_last_dim=PIECE)
+        nc.scalar.dma_start(q_codes[:], q_words.rearrange("b o p q t -> p (b o) (q t)").bitcast(I32))
         qs_rows = q_scales.rearrange("b o (g r) q -> r g (b o) q", r=4)
         for r in range(4):
-            nc.sync.dma_start(q_plane[r:P:32, :, :], qs_rows[r].bitcast(I32))
+            queue = nc.sync if r < 2 else nc.scalar
+            queue.dma_start(q_plane[r:P:32, :, :], qs_rows[r].bitcast(I32))
 
-        nc.vector.memset(ks_win[0:KS_ROW, :], 0)
+        vsc_got = keep.tile([P, PAGES * DV], U8, name="vsc_got")
+        nc.vector.tensor_copy(vsc_got[:], vsc_win[:].bitcast(U8).indirect(voffs_t[:]))
+
         ident = keep.tile([P, P], F32, name="ident")
         make_identity(nc, ident[:])
 
@@ -78,10 +84,8 @@ def tile_attend_pkv4_qpk_kernel(tc, q_words, q_scales, k_words, k_scales, v_word
         nc.vector.tensor_copy(ks_got[:], ks_win.bitcast(U8).indirect(offs_t[:]))
         k_plane = shared.tile([P, PASSES, B * N // 4], I32, name="k_plane", align_bytes=64, offset=KS_AT)
         for quad in (0, 2, 1, 3):
-            nc.sync.dma_start(k_plane[32 * quad : 32 * quad + 4, :, :], ks_got[KS_ROW + 8 * quad : KS_ROW + 8 * quad + 8, :].bitcast(I32))
+            nc.sync.dma_start(k_plane[32 * quad : 32 * quad + 4, :, :], ks_got[32 * quad : 32 * quad + 32 : KS_STEP, :].bitcast(I32))
 
-        vsc_got = keep.tile([P, PAGES * DV], U8, name="vsc_got")
-        nc.vector.tensor_copy(vsc_got[:], vsc_win[:].bitcast(U8).indirect(voffs_t[:]))
         vs_win = shared.tile([P, T], F32, name="vs_win", align_bytes=64, offset=VS_AT)
         nc.sync.dma_start(vs_win[:], vs, max_dma_last_dim=PIECE)
         vw_win = shared.tile([P, POOL_PAGES * DV], I32, name="vw_win", align_bytes=64, offset=VW_AT)
@@ -89,7 +93,7 @@ def tile_attend_pkv4_qpk_kernel(tc, q_words, q_scales, k_words, k_scales, v_word
             vw_win[:].rearrange("p (u e) -> p u e", u=POOL_PAGES),
             v_words.rearrange("u p e r -> p u (e r)").bitcast(I32),
         )
-        v_plane = shared.tile([P, PAGES * DV // 4], I32, name="v_plane", align_bytes=64, offset=VSC_AT)
+        v_plane = shared.tile([P, PAGES * DV // 4], I32, name="v_plane", align_bytes=64, offset=VP_AT)
         for quad in range(4):
             nc.sync.dma_start(
                 v_plane[32 * quad + V_PLANE : 32 * quad + V_PLANE + 4, :],
@@ -158,7 +162,7 @@ def tile_attend_pkv4_qpk_kernel(tc, q_words, q_scales, k_words, k_scales, v_word
             nc.vector.tensor_tensor(w32[g][:], vs_win[:].indirect(page_list(g)), p[g][:], ALU.mult)
         nc.scalar.copy(w16[1][:], w32[1][:])
         nc.scalar.copy(w16[2][:], w32[2][:])
-        nc.vector.tensor_copy(w16[3][:], w32[3][:])
+        nc.gpsimd.tensor_copy(w16[3][:], w32[3][:])
         bank = psum.tile([P, 4, NQ], F32, name="bank0", offset=4 * BANK)
         for t in range(4):
             nc.tensor.transpose(bank[:, t, :], w32[0][:, t:PAGE:4], ident[:])
@@ -189,22 +193,30 @@ def tile_attend_pkv4_qpk_kernel(tc, q_words, q_scales, k_words, k_scales, v_word
         quantise(2)
         v_got.append(gather_values(1, shared.tile([P, 2 * DV], U32, name="v_got1", align_bytes=64, offset=WT_AT + 2 * PAGE)))
         quantise(3)
-        for b in range(B):
-            acc = psum.tile([P, DV], F32, name="acc%d" % b, offset=(6 + b) * BANK)
+
+        def second_product(b, cols, bank_at):
+            width = cols.stop - cols.start
+            acc = psum.tile([P, width], F32, name="acc%d_%d" % (b, cols.start), offset=bank_at * BANK)
             for j in range(2):
                 g = 2 * b + j
                 nc.tensor.matmul_mx(
                     out=acc[:],
                     lhsT=w_codes[g][:].bitcast(FP8X4),
                     lhsT_scale=w_plane[g][:],
-                    rhs=v_got[b][:, j * DV : (j + 1) * DV].bitcast(FP8X4),
-                    rhs_scale=v_plane[V_PLANE:P, g * DV // 4 : (g + 1) * DV // 4].bitcast(U8),
+                    rhs=v_got[b][:, j * DV + cols.start : j * DV + cols.stop].bitcast(FP8X4),
+                    rhs_scale=v_plane[V_PLANE:P, (g * DV + cols.start) // 4 : (g * DV + cols.stop) // 4].bitcast(U8),
                     start=(j == 0),
                     stop=(j == 1),
                 )
-            y = keep.tile([P, DV], F32, name="y%d" % b)
-            if b == 0:
-                nc.scalar.activation(y[:], acc[:], ACT.Copy, scale=inv[:, b : b + 1])
-            else:
-                nc.vector.tensor_scalar(y[:], acc[:], inv[:, b : b + 1], None, ALU.mult)
-            nc.sync.dma_start(out[b], y[:])
+            return acc, keep.tile([P, width], F32, name="y%d_%d" % (b, cols.start))
+
+        acc, y = second_product(0, slice(0, DV), 6)
+        nc.scalar.activation(y[:], acc[:], ACT.Copy, scale=inv[:, 0:1])
+        nc.sync.dma_start(out[0], y[:])
+        low, high = slice(0, DV // 2), slice(DV // 2, DV)
+        acc, y = second_product(1, low, 7)
+        nc.scalar.activation(y[:], acc[:], ACT.Copy, scale=inv[:, 1:2])
+        nc.scalar.dma_start(out[1][:, low], y[:])
+        acc, y = second_product(1, high, 0)
+        nc.vector.tensor_scalar(y[:], acc[:], inv[:, 1:2], None, ALU.mult)
+        nc.sync.dma_start(out[1][:, high], y[:])

@@ -24,12 +24,10 @@ ACT = mybir.ActivationFunctionType
 
 V_PLANE = 4
 EDGE = 64
-VS_AT = 0
-KS_AT = VS_AT + 4 * T
+KS_AT = EDGE
 VP_AT = KS_AT + T
 VW_AT = VP_AT + PAGES * DV
-WT_AT = VW_AT + 4 * POOL_PAGES * DV
-VSC_AT = WT_AT + 5 * 2 * PAGE
+VSC_AT = VW_AT + 4 * POOL_PAGES * DV
 BANK = 2048
 PIECE = 4096
 VSC_ROW = 112
@@ -64,6 +62,8 @@ def tile_attend_pkv4_qpk_kernel(tc, q_words, q_scales, k_words, k_scales, v_word
             v_scales.rearrange("u f e -> f u e").bitcast(I32),
         )
         nc.sync.dma_start(offs_t[:], offs)
+        vs_slab = keep.tile([P, POOL_PAGES, 4], F32, name="vs_slab")
+        nc.sync.dma_start(vs_slab[:], vs[0].rearrange("(u p t) -> p u t", u=POOL_PAGES, t=4))
         kw_rows = k_words[0].rearrange("p t b -> p (t b)").bitcast(I32)
         nc.scalar.dma_start(kw_win[:, 0:KW_FIRST], kw_rows[:, 0:KW_FIRST])
         nc.scalar.dma_start(ks_win[0:P:KS_STEP, :], k_scales.rearrange("o f t -> f o t").bitcast(I32))
@@ -86,8 +86,14 @@ def tile_attend_pkv4_qpk_kernel(tc, q_words, q_scales, k_words, k_scales, v_word
         for quad in (0, 2, 1, 3):
             nc.sync.dma_start(k_plane[32 * quad : 32 * quad + 4, :, :], ks_got[32 * quad : 32 * quad + 32 : KS_STEP, :].bitcast(I32))
 
-        vs_win = shared.tile([P, T], F32, name="vs_win", align_bytes=64, offset=VS_AT)
-        nc.sync.dma_start(vs_win[:], vs, max_dma_last_dim=PIECE)
+        vs_win = keep.tile([P, T], F32, name="vs_win")
+        nc.scalar.activation(
+            vs_win[:].rearrange("p (u q t) -> p u q t", u=POOL_PAGES, t=4),
+            vs_slab[:].unsqueeze(2).to_broadcast([P, POOL_PAGES, NQ, 4]),
+            ACT.Copy,
+        )
+        vs_got = keep.tile([P, B * N], F32, name="vs_got")
+        nc.scalar.activation(vs_got[:], vs_win[:].indirect(offs_t[:]), ACT.Copy)
         vw_win = shared.tile([P, POOL_PAGES * DV], I32, name="vw_win", align_bytes=64, offset=VW_AT)
         nc.sync.dma_start(
             vw_win[:].rearrange("p (u e) -> p u e", u=POOL_PAGES),
@@ -105,7 +111,7 @@ def tile_attend_pkv4_qpk_kernel(tc, q_words, q_scales, k_words, k_scales, v_word
 
         scores = [psum.tile([P, PAGE], F32, name="scores%d" % g, offset=g * BANK) for g in range(PAGES)]
         k_got = {}
-        neg_score = [keep.tile([P, PAGE], F32, name="neg_score%d" % g) for g in range(PAGES)]
+        neg_score = [keep.tile([P, PAGE], F32, name="neg_score%d" % g, tag="neg_score%d" % g, align_bytes=64) for g in range(PAGES)]
         neg_max = [keep.tile([P, 1], F32, name="neg_max%d" % g) for g in range(PAGES)]
         p = [keep.tile([P, PAGE], F32, name="p%d" % g, tag="p%d" % g, align_bytes=64) for g in range(PAGES)]
         sums = keep.tile([P, 2, B], F32, name="sums")
@@ -131,7 +137,7 @@ def tile_attend_pkv4_qpk_kernel(tc, q_words, q_scales, k_words, k_scales, v_word
 
         def row_max(g):
             nc.vector.tensor_scalar(
-                neg_score[g][:], scores[g][:], -1.0, neg_max[g - 1][:] if g % 2 else None,
+                neg_score[g][:].rearrange("p (t s) -> p t s", t=4), scores[g][:].rearrange("p (s t) -> p t s", t=4), -1.0, neg_max[g - 1][:] if g % 2 else None,
                 ALU.mult, ALU.min, accum_out=neg_max[g][:],
             )
 
@@ -155,27 +161,22 @@ def tile_attend_pkv4_qpk_kernel(tc, q_words, q_scales, k_words, k_scales, v_word
         row_max(3)
         exps(1)
 
-        w_t = [shared.tile([P, PAGE], BF16, name="w_t%d" % g, align_bytes=64, offset=WT_AT + (0, 1, 3, 4)[g] * 2 * PAGE) for g in range(PAGES)]
-        w32 = [keep.tile([P, PAGE], F32, name="w32_%d" % g) for g in range(PAGES)]
-        w16 = {g: keep.tile([P, PAGE], BF16, name="w16_%d" % g) for g in range(1, PAGES)}
+        w_t = [keep.tile([P, PAGE], BF16, name="w_t%d" % g, align_bytes=64) for g in range(PAGES)]
+        turned = [psum.tile([P, 4, NQ], F32, name="turned%d" % g, offset=(4 + g) * BANK) for g in range(PAGES)]
         for g in range(PAGES):
-            nc.vector.tensor_tensor(w32[g][:], vs_win[:].indirect(page_list(g)), p[g][:], ALU.mult)
-        nc.scalar.copy(w16[1][:], w32[1][:])
-        nc.scalar.copy(w16[2][:], w32[2][:])
-        nc.gpsimd.tensor_copy(w16[3][:], w32[3][:])
-        bank = psum.tile([P, 4, NQ], F32, name="bank0", offset=4 * BANK)
-        for t in range(4):
-            nc.tensor.transpose(bank[:, t, :], w32[0][:, t:PAGE:4], ident[:])
-        nc.scalar.copy(w_t[0][:].rearrange("p (q t) -> p q t", t=4), bank[:].rearrange("p t q -> p q t"))
-        for g in range(1, PAGES):
-            bank = psum.tile([P, 2, NQ], F32, name="bank%d" % g, offset=(4 + g % 2) * BANK)
-            for u in range(2):
-                nc.tensor.transpose(bank[:, u, :], w16[g][:].bitcast(F32)[:, u : PAGE // 2 : 2], ident[:])
-            nc.scalar.copy(w_t[g][:].bitcast(F32).rearrange("p (q u) -> p q u", u=2), bank[:].rearrange("p u q -> p q u"))
+            for t in range(4):
+                nc.tensor.transpose(turned[g][:, t, :], p[g][:, t * NQ : (t + 1) * NQ], ident[:])
+
+        def weigh(g):
+            nc.vector.tensor_tensor(
+                w_t[g][:].rearrange("p (q t) -> p q t", t=4),
+                turned[g][:].rearrange("p t q -> p q t"),
+                vs_got[:, g * PAGE : (g + 1) * PAGE].rearrange("p (q t) -> p q t", t=4),
+                ALU.mult,
+            )
 
         total = keep.tile([P, B], F32, name="total")
         inv = keep.tile([P, B], F32, name="inv")
-        nc.vector.tensor_tensor(total[:], sums[:, 0, :], sums[:, 1, :], ALU.add)
         w_codes = [keep.tile([P, NQ], U32, name="w_codes%d" % g, align_bytes=64) for g in range(PAGES)]
         w_plane = [keep.tile([P, NQ], U8, name="w_plane%d" % g, align_bytes=64) for g in range(PAGES)]
 
@@ -186,12 +187,17 @@ def tile_attend_pkv4_qpk_kernel(tc, q_words, q_scales, k_words, k_scales, v_word
             nc.vector.tensor_copy(got[:], vw_win[:].bitcast(U32).indirect(voffs_t[:, b * 32 : (b + 1) * 32]))
             return got
 
-        v_got = [gather_values(0, keep.tile([P, 2 * DV], U32, name="v_got0", tag="p2", align_bytes=64))]
+        v_got = [gather_values(0, keep.tile([P, 2 * DV], U32, name="v_got0", tag="neg_score0", align_bytes=64))]
+        weigh(0)
+        weigh(1)
         quantise(0)
-        nc.vector.reciprocal(inv[:], total[:])
+        v_got.append(gather_values(1, keep.tile([P, 2 * DV], U32, name="v_got1", tag="neg_score2", align_bytes=64)))
         quantise(1)
+        nc.vector.tensor_tensor(total[:], sums[:, 0, :], sums[:, 1, :], ALU.add)
+        weigh(2)
+        nc.vector.reciprocal(inv[:], total[:])
+        weigh(3)
         quantise(2)
-        v_got.append(gather_values(1, shared.tile([P, 2 * DV], U32, name="v_got1", align_bytes=64, offset=WT_AT + 2 * PAGE)))
         quantise(3)
 
         def second_product(b, cols, bank_at):
@@ -210,13 +216,13 @@ def tile_attend_pkv4_qpk_kernel(tc, q_words, q_scales, k_words, k_scales, v_word
                 )
             return acc, keep.tile([P, width], F32, name="y%d_%d" % (b, cols.start))
 
-        acc, y = second_product(0, slice(0, DV), 6)
+        acc, y = second_product(0, slice(0, DV), 0)
         nc.scalar.activation(y[:], acc[:], ACT.Copy, scale=inv[:, 0:1])
         nc.sync.dma_start(out[0], y[:])
         low, high = slice(0, DV // 2), slice(DV // 2, DV)
-        acc, y = second_product(1, low, 7)
+        acc, y = second_product(1, low, 1)
         nc.scalar.activation(y[:], acc[:], ACT.Copy, scale=inv[:, 1:2])
         nc.scalar.dma_start(out[1][:, low], y[:])
-        acc, y = second_product(1, high, 0)
+        acc, y = second_product(1, high, 2)
         nc.vector.tensor_scalar(y[:], acc[:], inv[:, 1:2], None, ALU.mult)
         nc.sync.dma_start(out[1][:, high], y[:])

@@ -31,6 +31,7 @@ VSC_AT = VW_AT + 4 * POOL_PAGES * DV
 BANK = 2048
 PIECE = 4096
 VSC_ROW = 112
+VS_ROW = P - 1
 KS_STEP = 4
 KW_FIRST = PIECE // 4
 
@@ -47,14 +48,20 @@ def tile_attend_pkv4_qpk_kernel(tc, q_words, q_scales, k_words, k_scales, v_word
         voffs_t = lists.tile([P, PAGES * DV // 16], U16, name="voffs_t")
         ks_tile = shared.tile([P, (VW_AT - KS_AT + 2 * EDGE) // 4], I32, name="ks_tile", align_bytes=64, offset=KS_AT - EDGE)
         ks_win = ks_tile[:, EDGE // 4 : (EDGE + T) // 4]
-        vsc_win = shared.tile([P, POOL_PAGES * DV // 4], I32, name="vsc_win", align_bytes=64, offset=VSC_AT)
+        vsc_tile = shared.tile([P, POOL_PAGES * DV // 4 + 1], I32, name="vsc_tile", align_bytes=64, offset=VSC_AT)
+        vsc_win = vsc_tile[:, 0 : POOL_PAGES * DV // 4]
         kw_win = keep.tile([P, T], I32, name="kw_win")
         q_codes = keep.tile([P, B * PASSES, NQ], I32, name="q_codes", align_bytes=64)
-        q_plane = keep.tile([P, B * PASSES, NQ // 4], I32, name="q_plane", align_bytes=64)
-        nc.vector.memset(q_plane[:], 0)
+        q_tile = keep.tile([P, B * PASSES * NQ // 4 + 1], I32, name="q_tile", align_bytes=64)
+        q_plane = q_tile[:, 0 : B * PASSES * NQ // 4].rearrange("p (a q) -> p a q", a=B * PASSES)
+        vs_win = keep.tile([P, T], F32, name="vs_win")
+        ident = keep.tile([P, P], F32, name="ident")
         nc.gpsimd.memset(ks_win, 0)
-        nc.vector.memset(vsc_win[0:VSC_ROW, :], 0)
-        nc.vector.memset(ks_tile[:, (EDGE + T) // 4 : (EDGE + VW_AT - KS_AT) // 4], 0)
+        nc.gpsimd.memset(vs_win[0:VS_ROW, :], 0.0)
+        make_identity(nc, ident[:])
+        nc.vector.memset(q_tile[:], 0)
+        nc.vector.memset(vsc_tile[0:VSC_ROW, :], 0)
+        nc.vector.memset(ks_tile[:, (EDGE + T) // 4 : (EDGE + VW_AT - KS_AT) // 4 + 1], 0)
 
         nc.sync.dma_start(voffs_t[:], voffs)
         nc.scalar.dma_start(
@@ -62,8 +69,6 @@ def tile_attend_pkv4_qpk_kernel(tc, q_words, q_scales, k_words, k_scales, v_word
             v_scales.rearrange("u f e -> f u e").bitcast(I32),
         )
         nc.sync.dma_start(offs_t[:], offs)
-        vs_slab = keep.tile([P, POOL_PAGES, 4], F32, name="vs_slab")
-        nc.sync.dma_start(vs_slab[:], vs[0].rearrange("(u p t) -> p u t", u=POOL_PAGES, t=4))
         kw_rows = k_words[0].rearrange("p t b -> p (t b)").bitcast(I32)
         nc.scalar.dma_start(kw_win[:, 0:KW_FIRST], kw_rows[:, 0:KW_FIRST])
         nc.scalar.dma_start(ks_win[0:P:KS_STEP, :], k_scales.rearrange("o f t -> f o t").bitcast(I32))
@@ -71,14 +76,11 @@ def tile_attend_pkv4_qpk_kernel(tc, q_words, q_scales, k_words, k_scales, v_word
         nc.scalar.dma_start(q_codes[:], q_words.rearrange("b o p q t -> p (b o) (q t)").bitcast(I32))
         qs_rows = q_scales.rearrange("b o (g r) q -> r g (b o) q", r=4)
         for r in range(4):
-            queue = nc.sync if r < 2 else nc.scalar
-            queue.dma_start(q_plane[r:P:32, :, :], qs_rows[r].bitcast(I32))
+            nc.sync.dma_start(q_plane[r:P:32, :, :], qs_rows[r].bitcast(I32))
+        nc.scalar.dma_start(vs_win[VS_ROW:P, :], vs[0:1, :])
 
         vsc_got = keep.tile([P, PAGES * DV], U8, name="vsc_got")
-        nc.vector.tensor_copy(vsc_got[:], vsc_win[:].bitcast(U8).indirect(voffs_t[:]))
-
-        ident = keep.tile([P, P], F32, name="ident")
-        make_identity(nc, ident[:])
+        nc.vector.tensor_copy(vsc_got[:], vsc_win.bitcast(U8).indirect(voffs_t[:]))
 
         ks_got = keep.tile([P, B * N], U8, name="ks_got")
         nc.vector.tensor_copy(ks_got[:], ks_win.bitcast(U8).indirect(offs_t[:]))
@@ -86,14 +88,12 @@ def tile_attend_pkv4_qpk_kernel(tc, q_words, q_scales, k_words, k_scales, v_word
         for quad in (0, 2, 1, 3):
             nc.sync.dma_start(k_plane[32 * quad : 32 * quad + 4, :, :], ks_got[32 * quad : 32 * quad + 32 : KS_STEP, :].bitcast(I32))
 
-        vs_win = keep.tile([P, T], F32, name="vs_win")
-        nc.scalar.activation(
-            vs_win[:].rearrange("p (u q t) -> p u q t", u=POOL_PAGES, t=4),
-            vs_slab[:].unsqueeze(2).to_broadcast([P, POOL_PAGES, NQ, 4]),
-            ACT.Copy,
-        )
         vs_got = keep.tile([P, B * N], F32, name="vs_got")
-        nc.scalar.activation(vs_got[:], vs_win[:].indirect(offs_t[:]), ACT.Copy)
+        vs_col = [keep.tile([P, 4], F32, name="vs_col%d" % g) for g in range(PAGES)]
+        for b in range(B):
+            nc.scalar.activation(vs_got[:, b * N : (b + 1) * N], vs_win[:].indirect(offs_t[:, b * N // 16 : (b + 1) * N // 16]), ACT.Copy)
+            for g in (2 * b, 2 * b + 1):
+                nc.scalar.dma_start(vs_col[g][:], vs_got[VS_ROW:P, g * PAGE : (g + 1) * PAGE].rearrange("p (s t) -> p s t", t=4))
         vw_win = shared.tile([P, POOL_PAGES * DV], I32, name="vw_win", align_bytes=64, offset=VW_AT)
         nc.sync.dma_start(
             vw_win[:].rearrange("p (u e) -> p u e", u=POOL_PAGES),
@@ -137,14 +137,14 @@ def tile_attend_pkv4_qpk_kernel(tc, q_words, q_scales, k_words, k_scales, v_word
 
         def row_max(g):
             nc.vector.tensor_scalar(
-                neg_score[g][:].rearrange("p (t s) -> p t s", t=4), scores[g][:].rearrange("p (s t) -> p t s", t=4), -1.0, neg_max[g - 1][:] if g % 2 else None,
+                neg_score[g][:], scores[g][:], -1.0, neg_max[g - 1][:] if g % 2 else None,
                 ALU.mult, ALU.min, accum_out=neg_max[g][:],
             )
 
         def exps(b):
             for j in range(2):
                 g = 2 * b + j
-                nc.scalar.activation(p[g][:], neg_score[g][:], ACT.Exp, bias=neg_max[2 * b + 1][:], scale=-1.0, accum_out=sums[:, j, b : b + 1])
+                nc.scalar.activation(p[g][:].rearrange("p (t s) -> p s t", t=4), neg_score[g][:].rearrange("p (s t) -> p s t", t=4), ACT.Exp, bias=neg_max[2 * b + 1][:], scale=-1.0, accum_out=sums[:, j, b : b + 1])
 
         gather_keys(0)
         gather_keys(1)
@@ -171,7 +171,7 @@ def tile_attend_pkv4_qpk_kernel(tc, q_words, q_scales, k_words, k_scales, v_word
             nc.vector.tensor_tensor(
                 w_t[g][:].rearrange("p (q t) -> p q t", t=4),
                 turned[g][:].rearrange("p t q -> p q t"),
-                vs_got[:, g * PAGE : (g + 1) * PAGE].rearrange("p (q t) -> p q t", t=4),
+                vs_col[g][:].unsqueeze(1).to_broadcast([P, NQ, 4]),
                 ALU.mult,
             )
 

@@ -6,6 +6,7 @@ from concourse.masks import make_identity
 B, N, T, D, DV, NQ = 2, 1024, 4096, 1024, 256, 128
 PAGE = 512
 P = 128
+PACK = 4
 PASSES = D // 512
 PAGES = B * N // PAGE
 POOL_PAGES = T // PAGE
@@ -22,7 +23,6 @@ FP4X4 = mybir.dt.float4_e2m1fn_x4
 ALU = mybir.AluOpType
 ACT = mybir.ActivationFunctionType
 
-V_PLANE = 4
 EDGE = 64
 KS_AT = EDGE
 VP_AT = KS_AT + T
@@ -30,10 +30,12 @@ VW_AT = VP_AT + PAGES * DV
 VSC_AT = VW_AT + 4 * POOL_PAGES * DV
 BANK = 2048
 PIECE = 4096
-VSC_ROW = 112
-VS_ROW = P - 1
-KS_STEP = 4
 KW_FIRST = PIECE // 4
+KS_STEP = 4
+VSC_ROW = P - 16
+VS_ROW = P - 1
+V_PLANE = 4
+SCALAR_PAGE = 2
 
 
 def tile_attend_pkv4_qpk_kernel(tc, q_words, q_scales, k_words, k_scales, v_words, v_scales, vs, offs, voffs, out):
@@ -48,20 +50,24 @@ def tile_attend_pkv4_qpk_kernel(tc, q_words, q_scales, k_words, k_scales, v_word
         voffs_t = lists.tile([P, PAGES * DV // 16], U16, name="voffs_t")
         ks_tile = shared.tile([P, (VW_AT - KS_AT + 2 * EDGE) // 4], I32, name="ks_tile", align_bytes=64, offset=KS_AT - EDGE)
         ks_win = ks_tile[:, EDGE // 4 : (EDGE + T) // 4]
-        vsc_tile = shared.tile([P, POOL_PAGES * DV // 4 + 1], I32, name="vsc_tile", align_bytes=64, offset=VSC_AT)
-        vsc_win = vsc_tile[:, 0 : POOL_PAGES * DV // 4]
+        vsc_win = shared.tile([P, POOL_PAGES * DV // 4], I32, name="vsc_win", align_bytes=64, offset=VSC_AT)
         kw_win = keep.tile([P, T], I32, name="kw_win")
         q_codes = keep.tile([P, B * PASSES, NQ], I32, name="q_codes", align_bytes=64)
-        q_tile = keep.tile([P, B * PASSES * NQ // 4 + 1], I32, name="q_tile", align_bytes=64)
-        q_plane = q_tile[:, 0 : B * PASSES * NQ // 4].rearrange("p (a q) -> p a q", a=B * PASSES)
+        q_plane = keep.tile([P, B * PASSES, NQ // 4], I32, name="q_plane", align_bytes=64)
         vs_win = keep.tile([P, T], F32, name="vs_win")
         ident = keep.tile([P, P], F32, name="ident")
+
+        def clear_on_vector(words):
+            cut = words.shape[1] // 2 - 1
+            nc.vector.memset(words[:, 0:cut], 0)
+            nc.vector.memset(words[:, cut:], 0)
+
         nc.gpsimd.memset(ks_win, 0)
         nc.gpsimd.memset(vs_win[0:VS_ROW, :], 0.0)
         make_identity(nc, ident[:])
-        nc.vector.memset(q_tile[:], 0)
-        nc.vector.memset(vsc_tile[0:VSC_ROW, :], 0)
-        nc.vector.memset(ks_tile[:, (EDGE + T) // 4 : (EDGE + VW_AT - KS_AT) // 4 + 1], 0)
+        clear_on_vector(q_plane[:].rearrange("p a q -> p (a q)"))
+        clear_on_vector(vsc_win[0:VSC_ROW, :])
+        clear_on_vector(ks_tile[:, (VP_AT - KS_AT + EDGE) // 4 : (VW_AT - KS_AT + EDGE) // 4])
 
         nc.sync.dma_start(voffs_t[:], voffs)
         nc.scalar.dma_start(
@@ -80,7 +86,7 @@ def tile_attend_pkv4_qpk_kernel(tc, q_words, q_scales, k_words, k_scales, v_word
         nc.scalar.dma_start(vs_win[VS_ROW:P, :], vs[0:1, :])
 
         vsc_got = keep.tile([P, PAGES * DV], U8, name="vsc_got")
-        nc.vector.tensor_copy(vsc_got[:], vsc_win.bitcast(U8).indirect(voffs_t[:]))
+        nc.vector.tensor_copy(vsc_got[:], vsc_win[:].bitcast(U8).indirect(voffs_t[:]))
 
         ks_got = keep.tile([P, B * N], U8, name="ks_got")
         nc.vector.tensor_copy(ks_got[:], ks_win.bitcast(U8).indirect(offs_t[:]))
@@ -89,11 +95,11 @@ def tile_attend_pkv4_qpk_kernel(tc, q_words, q_scales, k_words, k_scales, v_word
             nc.sync.dma_start(k_plane[32 * quad : 32 * quad + 4, :, :], ks_got[32 * quad : 32 * quad + 32 : KS_STEP, :].bitcast(I32))
 
         vs_got = keep.tile([P, B * N], F32, name="vs_got")
-        vs_col = [keep.tile([P, 4], F32, name="vs_col%d" % g) for g in range(PAGES)]
+        vs_col = [keep.tile([P, PACK], F32, name="vs_col%d" % g) for g in range(PAGES)]
         for b in range(B):
             nc.scalar.activation(vs_got[:, b * N : (b + 1) * N], vs_win[:].indirect(offs_t[:, b * N // 16 : (b + 1) * N // 16]), ACT.Copy)
             for g in (2 * b, 2 * b + 1):
-                nc.scalar.dma_start(vs_col[g][:], vs_got[VS_ROW:P, g * PAGE : (g + 1) * PAGE].rearrange("p (s t) -> p s t", t=4))
+                nc.scalar.dma_start(vs_col[g][:], vs_got[VS_ROW:P, g * PAGE : (g + 1) * PAGE].rearrange("p (s t) -> p s t", t=PACK))
         vw_win = shared.tile([P, POOL_PAGES * DV], I32, name="vw_win", align_bytes=64, offset=VW_AT)
         nc.sync.dma_start(
             vw_win[:].rearrange("p (u e) -> p u e", u=POOL_PAGES),
@@ -106,9 +112,6 @@ def tile_attend_pkv4_qpk_kernel(tc, q_words, q_scales, k_words, k_scales, v_word
                 vsc_got[VSC_ROW + 4 * quad : VSC_ROW + 4 * quad + 4, :].bitcast(I32),
             )
 
-        def page_list(g):
-            return offs_t[:, g * PAGE // 16 : (g + 1) * PAGE // 16]
-
         scores = [psum.tile([P, PAGE], F32, name="scores%d" % g, offset=g * BANK) for g in range(PAGES)]
         k_got = {}
         neg_score = [keep.tile([P, PAGE], F32, name="neg_score%d" % g, tag="neg_score%d" % g, align_bytes=64) for g in range(PAGES)]
@@ -118,7 +121,7 @@ def tile_attend_pkv4_qpk_kernel(tc, q_words, q_scales, k_words, k_scales, v_word
 
         def gather_keys(g):
             k_got[g] = keep.tile([P, PAGE], U32, name="k_got%d" % g, tag="k_got%d" % (g % 2))
-            nc.vector.tensor_copy(k_got[g][:], kw_win[:].bitcast(U32).indirect(page_list(g)))
+            nc.vector.tensor_copy(k_got[g][:], kw_win[:].bitcast(U32).indirect(offs_t[:, g * PAGE // 16 : (g + 1) * PAGE // 16]))
 
         def score(g):
             b = g // 2
@@ -144,7 +147,10 @@ def tile_attend_pkv4_qpk_kernel(tc, q_words, q_scales, k_words, k_scales, v_word
         def exps(b):
             for j in range(2):
                 g = 2 * b + j
-                nc.scalar.activation(p[g][:].rearrange("p (t s) -> p s t", t=4), neg_score[g][:].rearrange("p (s t) -> p s t", t=4), ACT.Exp, bias=neg_max[2 * b + 1][:], scale=-1.0, accum_out=sums[:, j, b : b + 1])
+                nc.scalar.activation(
+                    p[g][:].rearrange("p (t s) -> p s t", t=PACK), neg_score[g][:].rearrange("p (s t) -> p s t", t=PACK),
+                    ACT.Exp, bias=neg_max[2 * b + 1][:], scale=-1.0, accum_out=sums[:, j, b : b + 1],
+                )
 
         gather_keys(0)
         gather_keys(1)
@@ -162,18 +168,24 @@ def tile_attend_pkv4_qpk_kernel(tc, q_words, q_scales, k_words, k_scales, v_word
         exps(1)
 
         w_t = [keep.tile([P, PAGE], BF16, name="w_t%d" % g, align_bytes=64) for g in range(PAGES)]
-        turned = [psum.tile([P, 4, NQ], F32, name="turned%d" % g, offset=(4 + g) * BANK) for g in range(PAGES)]
+        turned = [psum.tile([P, PACK, NQ], F32, name="turned%d" % g, offset=(PAGES + g) * BANK) for g in range(PAGES)]
         for g in range(PAGES):
-            for t in range(4):
+            for t in range(PACK):
                 nc.tensor.transpose(turned[g][:, t, :], p[g][:, t * NQ : (t + 1) * NQ], ident[:])
 
         def weigh(g):
             nc.vector.tensor_tensor(
-                w_t[g][:].rearrange("p (q t) -> p q t", t=4),
+                w_t[g][:].rearrange("p (q t) -> p q t", t=PACK),
                 turned[g][:].rearrange("p t q -> p q t"),
-                vs_col[g][:].unsqueeze(1).to_broadcast([P, NQ, 4]),
+                vs_col[g][:].unsqueeze(1).to_broadcast([P, NQ, PACK]),
                 ALU.mult,
             )
+
+        def weigh_on_scalar(g):
+            by_place = keep.tile([P, PACK, NQ], BF16, name="by_place", tag="y0_0")
+            for t in range(PACK):
+                nc.scalar.activation(by_place[:, t, :], turned[g][:, t, :], ACT.Copy, scale=vs_col[g][:, t : t + 1])
+            nc.scalar.copy(w_t[g][:].rearrange("p (q t) -> p q t", t=PACK), by_place[:].rearrange("p t q -> p q t"))
 
         total = keep.tile([P, B], F32, name="total")
         inv = keep.tile([P, B], F32, name="inv")
@@ -183,38 +195,40 @@ def tile_attend_pkv4_qpk_kernel(tc, q_words, q_scales, k_words, k_scales, v_word
         def quantise(g):
             nc.vector.quantize_mx(out=w_codes[g][:].bitcast(FP8X4), scales=w_plane[g][:], in_=w_t[g][:])
 
-        def gather_values(b, got):
-            nc.vector.tensor_copy(got[:], vw_win[:].bitcast(U32).indirect(voffs_t[:, b * 32 : (b + 1) * 32]))
+        def gather_values(b):
+            got = keep.tile([P, 2 * DV], U32, name="v_got%d" % b, tag="neg_score%d" % (2 * b), align_bytes=64)
+            nc.vector.tensor_copy(got[:], vw_win[:].bitcast(U32).indirect(voffs_t[:, b * 2 * DV // 16 : (b + 1) * 2 * DV // 16]))
             return got
 
-        v_got = [gather_values(0, keep.tile([P, 2 * DV], U32, name="v_got0", tag="neg_score0", align_bytes=64))]
+        v_got = [gather_values(0)]
         weigh(0)
         weigh(1)
+        weigh_on_scalar(SCALAR_PAGE)
         quantise(0)
-        v_got.append(gather_values(1, keep.tile([P, 2 * DV], U32, name="v_got1", tag="neg_score2", align_bytes=64)))
+        v_got.append(gather_values(1))
         quantise(1)
         nc.vector.tensor_tensor(total[:], sums[:, 0, :], sums[:, 1, :], ALU.add)
-        weigh(2)
-        nc.vector.reciprocal(inv[:], total[:])
         weigh(3)
-        quantise(2)
+        nc.vector.reciprocal(inv[:], total[:])
         quantise(3)
+        quantise(SCALAR_PAGE)
 
-        def second_product(b, cols, bank_at):
+        def second_product(b, cols, bank):
             width = cols.stop - cols.start
-            acc = psum.tile([P, width], F32, name="acc%d_%d" % (b, cols.start), offset=bank_at * BANK)
-            for j in range(2):
-                g = 2 * b + j
+            acc = psum.tile([P, width], F32, name="acc%d_%d" % (b, cols.start), offset=bank * BANK)
+            order = sorted((2 * b, 2 * b + 1), key=lambda g: g == SCALAR_PAGE)
+            for g in order:
+                j = g % 2
                 nc.tensor.matmul_mx(
                     out=acc[:],
                     lhsT=w_codes[g][:].bitcast(FP8X4),
                     lhsT_scale=w_plane[g][:],
                     rhs=v_got[b][:, j * DV + cols.start : j * DV + cols.stop].bitcast(FP8X4),
                     rhs_scale=v_plane[V_PLANE:P, (g * DV + cols.start) // 4 : (g * DV + cols.stop) // 4].bitcast(U8),
-                    start=(j == 0),
-                    stop=(j == 1),
+                    start=(g == order[0]),
+                    stop=(g == order[1]),
                 )
-            return acc, keep.tile([P, width], F32, name="y%d_%d" % (b, cols.start))
+            return acc, keep.tile([P, width], F32, name="y%d_%d" % (b, cols.start), tag="y%d_%d" % (b, cols.start))
 
         acc, y = second_product(0, slice(0, DV), 0)
         nc.scalar.activation(y[:], acc[:], ACT.Copy, scale=inv[:, 0:1])

@@ -140,7 +140,7 @@ def tile_attend_pkv4_qpk_kernel(tc, q_words, q_scales, k_words, k_scales, v_word
 
         def row_max(g):
             nc.vector.tensor_scalar(
-                neg_score[g][:], scores[g][:], -1.0, neg_max[g - 1][:] if g % 2 else None,
+                neg_score[g][:].rearrange("p (t s) -> p t s", t=PACK), scores[g][:].rearrange("p (s t) -> p t s", t=PACK), -1.0, neg_max[g - 1][:] if g % 2 else None,
                 ALU.mult, ALU.min, accum_out=neg_max[g][:],
             )
 
@@ -148,7 +148,7 @@ def tile_attend_pkv4_qpk_kernel(tc, q_words, q_scales, k_words, k_scales, v_word
             for j in range(2):
                 g = 2 * b + j
                 nc.scalar.activation(
-                    p[g][:].rearrange("p (t s) -> p s t", t=PACK), neg_score[g][:].rearrange("p (s t) -> p s t", t=PACK),
+                    p[g][:], neg_score[g][:],
                     ACT.Exp, bias=neg_max[2 * b + 1][:], scale=-1.0, accum_out=sums[:, j, b : b + 1],
                 )
 

from contextlib import ExitStack

import concourse.mybir as mybir
from concourse.masks import make_identity

B, N, T, D, DV, NQ = 2, 1024, 4096, 1024, 256, 128
PAGE = 512
P = 128
PACK = 4
PASSES = D // 512
PAGES = B * N // PAGE
POOL_PAGES = T // PAGE
FLOPS = 2 * B * NQ * N * (D + DV)

F32 = mybir.dt.float32
BF16 = mybir.dt.bfloat16
I32 = mybir.dt.int32
U32 = mybir.dt.uint32
U16 = mybir.dt.uint16
U8 = mybir.dt.uint8
FP8X4 = mybir.dt.float8_e4m3fn_x4
FP4X4 = mybir.dt.float4_e2m1fn_x4
ALU = mybir.AluOpType
ACT = mybir.ActivationFunctionType

EDGE = 64
KS_AT = EDGE
VP_AT = KS_AT + T
VW_AT = VP_AT + PAGES * DV
VSC_AT = VW_AT + 4 * POOL_PAGES * DV
BANK = 2048
PIECE = 4096
KW_FIRST = PIECE // 4
KS_STEP = 4
VSC_ROW = P - 16
VS_ROW = P - 1
V_PLANE = 4
SCALAR_PAGE = 2


def tile_attend_pkv4_qpk_kernel(tc, q_words, q_scales, k_words, k_scales, v_words, v_scales, vs, offs, voffs, out):
    nc = tc.nc
    with ExitStack() as ctx:
        lists = ctx.enter_context(tc.tile_pool(name="lists", bufs=1))
        keep = ctx.enter_context(tc.tile_pool(name="keep", bufs=1))
        shared = ctx.enter_context(tc.tile_pool(name="shared", bufs=1))
        psum = ctx.enter_context(tc.psum_pool(name="psum", bufs=1))

        offs_t = lists.tile([P, B * N // 16], U16, name="offs_t")
        voffs_t = lists.tile([P, PAGES * DV // 16], U16, name="voffs_t")
        ks_tile = shared.tile([P, (VW_AT - KS_AT + 2 * EDGE) // 4], I32, name="ks_tile", align_bytes=64, offset=KS_AT - EDGE)
        ks_win = ks_tile[:, EDGE // 4 : (EDGE + T) // 4]
        vsc_win = shared.tile([P, POOL_PAGES * DV // 4], I32, name="vsc_win", align_bytes=64, offset=VSC_AT)
        kw_win = keep.tile([P, T], I32, name="kw_win")
        q_codes = keep.tile([P, B * PASSES, NQ], I32, name="q_codes", align_bytes=64)
        q_plane = keep.tile([P, B * PASSES, NQ // 4], I32, name="q_plane", align_bytes=64)
        vs_win = keep.tile([P, T], F32, name="vs_win")
        ident = keep.tile([P, P], F32, name="ident")

        def clear_on_vector(words):
            cut = words.shape[1] // 2 - 1
            nc.vector.memset(words[:, 0:cut], 0)
            nc.vector.memset(words[:, cut:], 0)

        nc.gpsimd.memset(ks_win, 0)
        nc.gpsimd.memset(vs_win[0:VS_ROW, :], 0.0)
        make_identity(nc, ident[:])
        clear_on_vector(q_plane[:].rearrange("p a q -> p (a q)"))
        clear_on_vector(vsc_win[0:VSC_ROW, :])
        clear_on_vector(ks_tile[:, (VP_AT - KS_AT + EDGE) // 4 : (VW_AT - KS_AT + EDGE) // 4])

        nc.sync.dma_start(voffs_t[:], voffs)
        nc.scalar.dma_start(
            vsc_win[VSC_ROW:P, :].rearrange("p (u e) -> p u e", u=POOL_PAGES),
            v_scales.rearrange("u f e -> f u e").bitcast(I32),
        )
        nc.sync.dma_start(offs_t[:], offs)
        kw_rows = k_words[0].rearrange("p t b -> p (t b)").bitcast(I32)
        nc.scalar.dma_start(kw_win[:, 0:KW_FIRST], kw_rows[:, 0:KW_FIRST])
        nc.scalar.dma_start(ks_win[0:P:KS_STEP, :], k_scales.rearrange("o f t -> f o t").bitcast(I32))
        nc.scalar.dma_start(kw_win[:, KW_FIRST:T], kw_rows[:, KW_FIRST:T], max_dma_last_dim=PIECE)
        nc.scalar.dma_start(q_codes[:], q_words.rearrange("b o p q t -> p (b o) (q t)").bitcast(I32))
        qs_rows = q_scales.rearrange("b o (g r) q -> r g (b o) q", r=4)
        for r in range(4):
            nc.sync.dma_start(q_plane[r:P:32, :, :], qs_rows[r].bitcast(I32))
        nc.scalar.dma_start(vs_win[VS_ROW:P, :], vs[0:1, :])

        vsc_got = keep.tile([P, PAGES * DV], U8, name="vsc_got")
        nc.vector.tensor_copy(vsc_got[:], vsc_win[:].bitcast(U8).indirect(voffs_t[:]))

        ks_got = keep.tile([P, B * N], U8, name="ks_got")
        nc.vector.tensor_copy(ks_got[:], ks_win.bitcast(U8).indirect(offs_t[:]))
        k_plane = shared.tile([P, PASSES, B * N // 4], I32, name="k_plane", align_bytes=64, offset=KS_AT)
        for quad in (0, 2, 1, 3):
            nc.sync.dma_start(k_plane[32 * quad : 32 * quad + 4, :, :], ks_got[32 * quad : 32 * quad + 32 : KS_STEP, :].bitcast(I32))

        vs_got = keep.tile([P, B * N], F32, name="vs_got")
        vs_col = [keep.tile([P, PACK], F32, name="vs_col%d" % g) for g in range(PAGES)]
        for b in range(B):
            nc.scalar.activation(vs_got[:, b * N : (b + 1) * N], vs_win[:].indirect(offs_t[:, b * N // 16 : (b + 1) * N // 16]), ACT.Copy)
            for g in (2 * b, 2 * b + 1):
                nc.scalar.dma_start(vs_col[g][:], vs_got[VS_ROW:P, g * PAGE : (g + 1) * PAGE].rearrange("p (s t) -> p s t", t=PACK))
        vw_win = shared.tile([P, POOL_PAGES * DV], I32, name="vw_win", align_bytes=64, offset=VW_AT)
        nc.sync.dma_start(
            vw_win[:].rearrange("p (u e) -> p u e", u=POOL_PAGES),
            v_words.rearrange("u p e r -> p u (e r)").bitcast(I32),
        )
        v_plane = shared.tile([P, PAGES * DV // 4], I32, name="v_plane", align_bytes=64, offset=VP_AT)
        for quad in range(4):
            nc.sync.dma_start(
                v_plane[32 * quad + V_PLANE : 32 * quad + V_PLANE + 4, :],
                vsc_got[VSC_ROW + 4 * quad : VSC_ROW + 4 * quad + 4, :].bitcast(I32),
            )

        scores = [psum.tile([P, PAGE], F32, name="scores%d" % g, offset=g * BANK) for g in range(PAGES)]
        k_got = {}
        neg_score = [keep.tile([P, PAGE], F32, name="neg_score%d" % g, tag="neg_score%d" % g, align_bytes=64) for g in range(PAGES)]
        neg_max = [keep.tile([P, 1], F32, name="neg_max%d" % g) for g in range(PAGES)]
        p = [keep.tile([P, PAGE], F32, name="p%d" % g, tag="p%d" % g, align_bytes=64) for g in range(PAGES)]
        sums = keep.tile([P, 2, B], F32, name="sums")

        def gather_keys(g):
            k_got[g] = keep.tile([P, PAGE], U32, name="k_got%d" % g, tag="k_got%d" % (g % 2))
            nc.vector.tensor_copy(k_got[g][:], kw_win[:].bitcast(U32).indirect(offs_t[:, g * PAGE // 16 : (g + 1) * PAGE // 16]))

        def score(g):
            b = g // 2
            k_pass = keep.tile([P, PASSES, 2 * PAGE], U8, name="k_pass%d" % g, tag="k_pass%d" % (g % 3), align_bytes=64)
            nc.vector.tensor_copy(k_pass[:].bitcast(U16), k_got[g][:].bitcast(U16).rearrange("p (n o) -> p o n", o=PASSES))
            for o in range(PASSES):
                nc.tensor.matmul_mx(
                    out=scores[g][:],
                    lhsT=q_codes[:, b * PASSES + o, :].bitcast(FP8X4),
                    lhsT_scale=q_plane[:, b * PASSES + o, :].bitcast(U8),
                    rhs=k_pass[:, o, :].bitcast(FP4X4),
                    rhs_scale=k_plane[:, o, g * PAGE // 4 : (g + 1) * PAGE // 4].bitcast(U8),
                    start=(o == 0),
                    stop=(o == PASSES - 1),
                )

        def row_max(g):
            nc.vector.tensor_scalar(
                neg_score[g][:].rearrange("p (t s) -> p t s", t=PACK), scores[g][:].rearrange("p (s t) -> p t s", t=PACK), -1.0, neg_max[g - 1][:] if g % 2 else None,
                ALU.mult, ALU.min, accum_out=neg_max[g][:],
            )

        def exps(b):
            for j in range(2):
                g = 2 * b + j
                nc.scalar.activation(
                    p[g][:], neg_score[g][:],
                    ACT.Exp, bias=neg_max[2 * b + 1][:], scale=-1.0, accum_out=sums[:, j, b : b + 1],
                )

        gather_keys(0)
        gather_keys(1)
        score(0)
        score(1)
        gather_keys(2)
        gather_keys(3)
        score(2)
        row_max(0)
        score(3)
        row_max(1)
        exps(0)
        row_max(2)
        row_max(3)
        exps(1)

        w_t = [keep.tile([P, PAGE], BF16, name="w_t%d" % g, align_bytes=64) for g in range(PAGES)]
        turned = [psum.tile([P, PACK, NQ], F32, name="turned%d" % g, offset=(PAGES + g) * BANK) for g in range(PAGES)]
        for g in range(PAGES):
            for t in range(PACK):
                nc.tensor.transpose(turned[g][:, t, :], p[g][:, t * NQ : (t + 1) * NQ], ident[:])

        def weigh(g):
            nc.vector.tensor_tensor(
                w_t[g][:].rearrange("p (q t) -> p q t", t=PACK),
                turned[g][:].rearrange("p t q -> p q t"),
                vs_col[g][:].unsqueeze(1).to_broadcast([P, NQ, PACK]),
                ALU.mult,
            )

        def weigh_on_scalar(g):
            by_place = keep.tile([P, PACK, NQ], BF16, name="by_place", tag="y0_0")
            for t in range(PACK):
                nc.scalar.activation(by_place[:, t, :], turned[g][:, t, :], ACT.Copy, scale=vs_col[g][:, t : t + 1])
            nc.scalar.copy(w_t[g][:].rearrange("p (q t) -> p q t", t=PACK), by_place[:].rearrange("p t q -> p q t"))

        total = keep.tile([P, B], F32, name="total")
        inv = keep.tile([P, B], F32, name="inv")
        w_codes = [keep.tile([P, NQ], U32, name="w_codes%d" % g, align_bytes=64) for g in range(PAGES)]
        w_plane = [keep.tile([P, NQ], U8, name="w_plane%d" % g, align_bytes=64) for g in range(PAGES)]

        def quantise(g):
            nc.vector.quantize_mx(out=w_codes[g][:].bitcast(FP8X4), scales=w_plane[g][:], in_=w_t[g][:])

        def gather_values(b):
            got = keep.tile([P, 2 * DV], U32, name="v_got%d" % b, tag="neg_score%d" % (2 * b), align_bytes=64)
            nc.vector.tensor_copy(got[:], vw_win[:].bitcast(U32).indirect(voffs_t[:, b * 2 * DV // 16 : (b + 1) * 2 * DV // 16]))
            return got

        v_got = [gather_values(0)]
        weigh(0)
        weigh(1)
        weigh_on_scalar(SCALAR_PAGE)
        quantise(0)
        v_got.append(gather_values(1))
        quantise(1)
        nc.vector.tensor_tensor(total[:], sums[:, 0, :], sums[:, 1, :], ALU.add)
        weigh(3)
        nc.vector.reciprocal(inv[:], total[:])
        quantise(3)
        quantise(SCALAR_PAGE)

        def second_product(b, cols, bank):
            width = cols.stop - cols.start
            acc = psum.tile([P, width], F32, name="acc%d_%d" % (b, cols.start), offset=bank * BANK)
            order = sorted((2 * b, 2 * b + 1), key=lambda g: g == SCALAR_PAGE)
            for g in order:
                j = g % 2
                nc.tensor.matmul_mx(
                    out=acc[:],
                    lhsT=w_codes[g][:].bitcast(FP8X4),
                    lhsT_scale=w_plane[g][:],
                    rhs=v_got[b][:, j * DV + cols.start : j * DV + cols.stop].bitcast(FP8X4),
                    rhs_scale=v_plane[V_PLANE:P, (g * DV + cols.start) // 4 : (g * DV + cols.stop) // 4].bitcast(U8),
                    start=(g == order[0]),
                    stop=(g == order[1]),
                )
            return acc, keep.tile([P, width], F32, name="y%d_%d" % (b, cols.start), tag="y%d_%d" % (b, cols.start))

        acc, y = second_product(0, slice(0, DV), 0)
        nc.scalar.activation(y[:], acc[:], ACT.Copy, scale=inv[:, 0:1])
        nc.sync.dma_start(out[0], y[:])
        low, high = slice(0, DV // 2), slice(DV // 2, DV)
        acc, y = second_product(1, low, 1)
        nc.scalar.activation(y[:], acc[:], ACT.Copy, scale=inv[:, 1:2])
        nc.scalar.dma_start(out[1][:, low], y[:])
        acc, y = second_product(1, high, 2)
        nc.vector.tensor_scalar(y[:], acc[:], inv[:, 1:2], None, ALU.mult)
        nc.sync.dma_start(out[1][:, high], y[:])
